import numpy as np
import ml_dtypes


def mxq(x, axis, fmt="e4m3"):
    dtype, down = {"e4m3": (ml_dtypes.float8_e4m3fn, 7), "e5m2": (ml_dtypes.float8_e5m2, 14)}[fmt]
    v = np.moveaxis(np.asarray(x, np.float32).astype(ml_dtypes.bfloat16).astype(np.float64), axis, -1)
    blocks = v.reshape(v.shape[:-1] + (-1, 32))
    amax = np.abs(blocks).max(-1, keepdims=True)
    byte = np.maximum(np.where(amax > 0, np.frexp(amax)[1] - 1 + 127, 0) - down, 1)
    scale = np.exp2(byte - 127.0)
    codes = (blocks / scale).astype(np.float32).astype(dtype).astype(np.float64)
    return np.moveaxis((codes * scale).reshape(v.shape), -1, axis)


WIDE = False


def mx_kscale(k):
    if not WIDE:
        return np.ones(k)
    levels = np.array([10, -10, 5, -5, 0])
    if k % 512:
        return np.exp2(np.random.permutation(np.resize(levels, k // 32))).repeat(32)
    a = np.empty((k // 512, 16))
    for p in range(k // 512):
        a[p, :8] = np.random.permutation(np.resize(levels, 8))
        for g in range(8):
            far = levels[np.abs(levels - a[p, g]) >= 10]
            a[p, g + 8] = far[np.random.randint(len(far))]
    return np.exp2(a.ravel()).repeat(32)


def f64(x):
    return np.asarray(x).astype(np.float64)


def striped(idx):
    return np.tile(idx.reshape(-1, 16).T, (8, 1)).astype(np.uint16)


def unstriped(offs):
    return offs[:16].T.reshape(-1).astype(np.int64)


E2M1 = np.array([0.0, 0.5, 1.0, 1.5, 2.0, 3.0, 4.0, 6.0, -0.0, -0.5, -1.0, -1.5, -2.0, -3.0, -4.0, -6.0])


def pack_weight(w, fmt):
    k, n = w.shape
    w = f64(np.asarray(w, np.float32).astype(ml_dtypes.bfloat16)).reshape(k // 32, 32, n)
    amax = np.abs(w).max(1)
    if fmt == "e4m3":
        byte = np.frexp(amax)[1] - 1 + 127 - 7
    else:
        mant, ex = np.frexp(amax / 6.0)
        byte = np.where(mant > 0.5, ex, ex - 1) + 127
    byte = np.clip(np.where(amax > 0, byte, 1), 1, 254)
    scaled = (w * np.exp2(127.0 - byte)[:, None, :]).reshape(k, n).astype(np.float32)
    by_word = np.ascontiguousarray(scaled.reshape(k // 512, 128, 4, n).transpose(0, 1, 3, 2))
    if fmt == "e4m3":
        words = by_word.astype(ml_dtypes.float8_e4m3fn).view(np.uint8)
    else:
        c = by_word.astype(ml_dtypes.float4_e2m1fn).view(np.uint8) & 0xF
        words = (c[..., 0::2] | (c[..., 1::2] << 4)).reshape(k // 512, 128, 2 * n)
    return np.ascontiguousarray(words), np.ascontiguousarray(byte.astype(np.uint8).reshape(k // 512, 16, n))


def unpack_weight(words, scales, fmt):
    g, _, n = scales.shape
    words = np.ascontiguousarray(words).reshape(g, 128, n, -1)
    if fmt == "e4m3":
        vals = words.view(ml_dtypes.float8_e4m3fn).astype(np.float64)
    else:
        nib = np.empty((g, 128, n, 4), np.uint8)
        nib[..., 0::2] = words & 0xF
        nib[..., 1::2] = words >> 4
        vals = E2M1[nib]
    vals = vals * np.repeat(np.exp2(scales.astype(np.float64) - 127.0), 8, axis=1)[..., None]
    return vals.transpose(0, 1, 3, 2).reshape(g * 512, n)


def gelu(v):
    return 0.5 * v * (1.0 + np.tanh(np.sqrt(2.0 / np.pi) * (v + 0.044715 * v**3)))


def bf(x):
    return np.asarray(x, np.float32).astype(ml_dtypes.bfloat16)


def planes(Y):
    n, m = Y.shape
    b = f64(bf(Y)).reshape(n // 32, 32, m)
    amax = np.abs(b).max(1)
    byte = np.clip(np.where(amax > 0, np.frexp(amax)[1] - 1 + 127 - 7, 1), 1, 254)
    codes = (b * np.exp2(127.0 - byte)[:, None, :]).reshape(n, m).astype(np.float32).astype(ml_dtypes.float8_e4m3fn).view(np.uint8)
    words = codes.reshape(n // 512, 128, 4, m).transpose(0, 1, 3, 2)
    return np.ascontiguousarray(words), np.ascontiguousarray(byte.astype(np.uint8).reshape(n // 512, 16, m))


K, T, S, H, T2, N = 512, 4096, 1024, 1024, 2048, 384

def setup_inputs():
    n = np.random.standard_normal
    s = mx_kscale(K)[:, None]
    u = mx_kscale(H)[:, None]
    tab_words, tab_scales = pack_weight(n((K, T)) * s, "e4m3")
    w1_words, w1_scales = pack_weight(n((K, H)) / np.sqrt(K) / s * u.T, "e2m1")
    w2 = n((K, H)) / np.sqrt(K) / s * u.T
    w3_words, w3_scales = pack_weight(n((H, N)) / np.sqrt(H) / u, "e4m3")
    return {
        "tab_words": tab_words, "tab_scales": tab_scales,
        "offs": striped(np.random.permutation(T)[:S]),
        "offs2": striped(np.random.permutation(T2)[:S]),
        "w1_words": w1_words, "w1_scales": w1_scales,
        "w2": w2.astype(np.float32),
        "w3_words": w3_words, "w3_scales": w3_scales,
        "c0": (np.random.uniform(0.3, 1.2, H) * u[:, 0] ** 2).astype(np.float32),
        "wgs": np.exp(0.3 * n((128, S))).astype(np.float32),
        "page0": (n((H, T2)) * u).astype(np.float32),
        "vis": np.random.uniform(0.25, 1.0, (N, T2)).astype(np.float32),
    }

def reference(tab_words, tab_scales, offs, offs2, w1_words, w1_scales, w2, w3_words, w3_scales, c0, wgs, page0, vis):
    v = unpack_weight(tab_words, tab_scales, "e4m3")[:, unstriped(offs)]
    w1 = unpack_weight(w1_words, w1_scales, "e2m1")
    w3 = unpack_weight(w3_words, w3_scales, "e4m3")
    a = w1.T @ v
    b = mxq(f64(w2), 0, "e4m3").T @ v
    h = np.sqrt(np.square(a) + np.square(b) + f64(c0)[:, None])
    page = f64(page0).copy()
    page[:, unstriped(offs2)] = np.tile(f64(wgs), (H // 128, 1)) * h
    words, scales = planes(page)
    y = f64(vis) * (w3.T @ mxq(page, 0, "e4m3"))
    return y, page, words, scales

@@ -1,0 +1,312 @@
+from contextlib import ExitStack
+
+import concourse.mybir as mybir
+from concourse.masks import make_identity
+
+K, T, S, H, T2, N = 512, 4096, 1024, 1024, 2048, 384
+FLOPS = 2 * (2 * K * H * S + H * N * T2)
+
+F32 = mybir.dt.float32
+BF16 = mybir.dt.bfloat16
+I32 = mybir.dt.int32
+U32 = mybir.dt.uint32
+U16 = mybir.dt.uint16
+U8 = mybir.dt.uint8
+FP8X4 = mybir.dt.float8_e4m3fn_x4
+FP4X4 = mybir.dt.float4_e2m1fn_x4
+MULT = mybir.AluOpType.mult
+SQUARE = mybir.ActivationFunctionType.Square
+SQRT = mybir.ActivationFunctionType.Sqrt
+
+P = 128
+BANK = 512
+TILES = H // P
+GROUPS = H // 512
+CHUNKS = T2 // BANK
+NBLOCKS = N // P
+W2_PIECES = ((0, 256), (256, 512), (512, 768), (768, 1024))
+
+
+def tile_list_floorplan_beacon_tiles_kernel(
+    tc, tab_words, tab_scales, offs, offs2, w1_words, w1_scales, w2, w3_words, w3_scales, c0, wgs, page0, vis,
+    out_0, out_1, out_2, out_3,
+):
+    nc = tc.nc
+    with ExitStack() as ctx:
+        lists = ctx.enter_context(tc.tile_pool(name="lists", bufs=1))
+        sb = ctx.enter_context(tc.tile_pool(name="sb", bufs=1))
+        ps = ctx.enter_context(tc.psum_pool(name="ps", bufs=1))
+
+        def tiles(name, count, shape, dtype):
+            return [sb.tile(shape, dtype, name=name + str(i), align_bytes=64) for i in range(count)]
+
+        pick = lists.tile([P, S // 16], U16, name="pick")
+        place = lists.tile([P, S // 16], U16, name="place")
+        banks = [ps.tile([P, BANK], F32, name="bank" + str(i)) for i in range(8)]
+
+        tab_w = sb.tile([P, T], I32, name="tab_w", align_bytes=64)
+        tab_s = sb.tile([P, T], U8, name="tab_s", align_bytes=64)
+        v_w = tiles("v_w", 2, [P, S // 2], U32)
+        v_s = tiles("v_s", 2, [P, S // 2], U8)
+        w1_w = sb.tile([P, 2 * H], U8, name="w1_w", align_bytes=64)
+        w1_s = sb.tile([P, H], U8, name="w1_s", align_bytes=64)
+        w2_raw = [sb.tile([P, 4, b - a], F32, name="w2_raw" + str(a), align_bytes=64) for a, b in W2_PIECES]
+        w2_bf = tiles("w2_bf", len(W2_PIECES), [P, 2 * BANK], BF16)
+        w2_w = sb.tile([P, H], U32, name="w2_w", align_bytes=64)
+        w2_s = sb.tile([P, H], U8, name="w2_s", align_bytes=64)
+        w3_w = sb.tile([P, GROUPS * N], I32, name="w3_w", align_bytes=64)
+        w3_s = sb.tile([P, GROUPS * N], U8, name="w3_s", align_bytes=64)
+        c0_rows = sb.tile([P, P], F32, name="c0_rows", align_bytes=64)
+        c0_cols = sb.tile([P, TILES], F32, name="c0_cols", align_bytes=64)
+        ident = sb.tile([P, P], F32, name="ident", align_bytes=64)
+        warm = tiles("warm", 2, [P, 1], F32)
+        wgs_sb = sb.tile([P, S], F32, name="wgs_sb", align_bytes=64)
+        pages = tiles("page", TILES, [P, T2], F32)
+        vis_sb = tiles("vis", NBLOCKS, [P, T2], F32)
+        squares = tiles("squares", 4, [P, BANK], F32)
+        hs = tiles("h", 2, [P, S], F32)
+        turned = tiles("turned", CHUNKS, [P, 4 * BANK], BF16)
+        grouped = tiles("grouped", 3, [P, 4 * BANK], BF16)
+        codes = tiles("codes", GROUPS, [P, T2], U32)
+        scales = tiles("scales", GROUPS, [P, T2], U8)
+
+        nc.vector.memset(tab_s[:].bitcast(I32), 0)
+        nc.gpsimd.memset(w1_s[:].bitcast(I32), 0)
+        nc.gpsimd.memset(c0_rows[:], 0.0)
+        nc.vector.memset(warm[0][:], 1.0)
+        nc.vector.memset(w3_s[:].bitcast(I32), 0)
+        make_identity(nc, ident[:])
+        nc.scalar.activation(warm[1][:], warm[0][:], SQRT)
+
+        def load_w2(i):
+            a, b = W2_PIECES[i]
+            nc.sync.dma_start(w2_raw[i][:], w2[:, a:b].rearrange("(p i) c -> p i c", i=4))
+
+        def load_w1(half):
+            cols = slice(half * H // 4, (half + 1) * H // 4)
+            nc.sync.dma_start(w1_w[:].bitcast(I32)[:, cols], w1_words[0].bitcast(I32)[:, cols])
+
+        def load_page(s):
+            nc.sync.dma_start(pages[s][:], page0[s * P:(s + 1) * P, :])
+
+        nc.sync.dma_start(pick[:], offs)
+        nc.sync.dma_start(place[:], offs2)
+        load_w1(0)
+        for r in range(4):
+            nc.gpsimd.dma_start(tab_s[r:P:32, :].bitcast(I32), tab_scales[0, r:16:4, :].bitcast(I32))
+        load_w2(0)
+        nc.sync.dma_start(tab_w[:], tab_words[0].rearrange("p t i -> p (t i)").bitcast(I32))
+        for r in range(4):
+            nc.scalar.dma_start(w1_s[r:P:32, :].bitcast(I32), w1_scales[0, r:16:4, :].bitcast(I32))
+        nc.scalar.dma_start(c0_rows[0:TILES, :], c0.rearrange("(s p) -> s p", p=P))
+        nc.sync.dma_start(wgs_sb[:], wgs)
+        load_page(0)
+        load_w2(1)
+        load_page(1)
+        load_w2(2)
+        load_w1(1)
+        load_page(2)
+        load_w2(3)
+        for s in range(3, TILES):
+            load_page(s)
+        nc.sync.dma_start(
+            w3_w[:].rearrange("p (g n) -> p g n", g=GROUPS),
+            w3_words.rearrange("g p n t -> p g (n t)").bitcast(I32),
+        )
+        for r in range(4):
+            nc.sync.dma_start(
+                w3_s[r:P:32, :].bitcast(I32).rearrange("q (g n) -> q g n", g=GROUPS),
+                w3_scales.bitcast(I32)[:, r:16:4, :].rearrange("g q n -> q g n"),
+            )
+        for b in range(NBLOCKS):
+            nc.sync.dma_start(vis_sb[b][:], vis[b * P:(b + 1) * P, :])
+
+        nc.tensor.transpose(banks[7][:, 0:P], c0_rows[:], ident[:])
+        nc.scalar.copy(c0_cols[:], banks[7][:, 0:TILES])
+
+        def quantize_w2(i):
+            a, b = W2_PIECES[i]
+            rounded = w2_bf[i][:, 0:4 * (b - a)]
+            nc.scalar.copy(
+                rounded.rearrange("p (c i t) -> p c t i", i=4, t=4),
+                w2_raw[i][:].rearrange("p t (c i) -> p c t i", i=4),
+            )
+            nc.vector.quantize_mx(w2_w[:, a:b].bitcast(FP8X4), w2_s[:, a:b], rounded)
+
+        quantize_w2(0)
+        for half in range(2):
+            entries = pick[:, 32 * half:32 * (half + 1)]
+            nc.vector.tensor_copy(v_w[half][:], tab_w[:].bitcast(U32).indirect(entries))
+            nc.vector.tensor_copy(v_s[half][:], tab_s[:].indirect(entries))
+
+        ring = {"work": 2, "sum": 0, "square": 0, "grouped": 0}
+
+        def take(kind, items):
+            item = items[ring[kind] % len(items)]
+            ring[kind] = ring[kind] + 1
+            return item
+
+        work_banks = [banks[0], banks[1], banks[2]]
+        sum_banks = [banks[3], banks[4], banks[7]]
+
+        def magnitudes(s, j_from, j_to, product_banks, total, last_squares=None):
+            r_cols = slice(s * P, (s + 1) * P)
+            made = []
+            for j0, bank in zip(range(j_from, j_to, 2 * P), product_banks):
+                for i in range(2):
+                    j = j0 + i * P
+                    words = v_w[j // BANK][:, j % BANK:j % BANK + P].bitcast(FP8X4)
+                    plane = v_s[j // BANK][:, j % BANK:j % BANK + P]
+                    nc.tensor.matmul_mx(
+                        bank[:, (2 * i) * P:(2 * i + 1) * P], lhsT=words, lhsT_scale=plane,
+                        rhs=w1_w[:, 2 * s * P:2 * (s + 1) * P].bitcast(FP4X4), rhs_scale=w1_s[:, r_cols],
+                        start=True, stop=True,
+                    )
+                    nc.tensor.matmul_mx(
+                        bank[:, (2 * i + 1) * P:(2 * i + 2) * P], lhsT=words, lhsT_scale=plane,
+                        rhs=w2_w[:, r_cols].bitcast(FP8X4), rhs_scale=w2_s[:, r_cols],
+                        start=True, stop=True,
+                    )
+                if last_squares is not None and j0 + 2 * P == j_to:
+                    sq = last_squares
+                else:
+                    sq = take("square", squares)[:]
+                nc.scalar.activation(sq, bank[:], SQUARE)
+                made.append(sq)
+            for n, sq in enumerate(made):
+                for i in range(2):
+                    dst = total[:, (2 * n + i) * P:(2 * n + i + 1) * P]
+                    for part in range(2):
+                        nc.tensor.matmul(
+                            dst, lhsT=sq[:, (2 * i + part) * P:(2 * i + part + 1) * P], rhs=ident[:],
+                            start=(part == 0), stop=(part == 1), is_transpose=True,
+                        )
+            nc.scalar.activation(hs[s % 2][:, j_from:j_to], total[:, 0:j_to - j_from], SQRT, bias=c0_cols[:, s:s + 1])
+
+        def scatter(s, j_from, j_to):
+            nc.vector.tensor_tensor(
+                pages[s][:].indirect(place[:, j_from // 16:j_to // 16]),
+                hs[s % 2][:, j_from:j_to], wgs_sb[:, j_from:j_to], MULT,
+            )
+
+        def store_page(s):
+            nc.sync.dma_start(out_1[s * P:(s + 1) * P, :], pages[s][:])
+
+        def turn(s, c, copy):
+            bank = take("work", work_banks)
+            for mb in range(4):
+                m0 = c * BANK + mb * P
+                nc.tensor.transpose(bank[:, mb * P:(mb + 1) * P], pages[s][:, m0:m0 + P], ident[:])
+            q0 = 32 * (s % 4)
+            copy(
+                turned[c][:].rearrange("m (b u p e) -> m b u p e", b=4, u=2, e=2)[:, :, :, q0:q0 + 32, :],
+                bank[:].rearrange("m (b q u e) -> m b u q e", b=4, u=2, e=2),
+            )
+
+        def turn_back(g, c, copies):
+            ready = take("grouped", grouped)
+            words = turned[c][:].bitcast(F32)
+            for half in range(2):
+                bank = banks[5 + half]
+                for i in range(4):
+                    w0 = (4 * half + i) * P
+                    nc.tensor.transpose(bank[:, i * P:(i + 1) * P], words[:, w0:w0 + P], ident[:])
+                copies[half](
+                    ready[:].bitcast(F32)[:, half * BANK:(half + 1) * BANK].rearrange("p (b m u) -> p b m u", b=2, u=2),
+                    bank[:].rearrange("p (b u m) -> p b m u", b=2, u=2),
+                )
+            cols = slice(c * BANK, (c + 1) * BANK)
+            nc.vector.quantize_mx(codes[g][:, cols].bitcast(FP8X4), scales[g][:, cols], ready[:])
+
+        def store_codes(g, c_from, c_to):
+            cols = slice(c_from * BANK, c_to * BANK)
+            nc.sync.dma_start(
+                out_2[g].rearrange("p m t -> p (m t)").bitcast(I32)[:, cols], codes[g][:, cols].bitcast(I32)
+            )
+
+        def store_scales(g):
+            for r in range(4):
+                nc.sync.dma_start(out_3[g, r:16:4, :].bitcast(I32), scales[g][r:P:32, :].bitcast(I32))
+
+        def readout_pass(g, c, b):
+            bank = (sum_banks if c % 2 == 0 else work_banks)[b]
+            cols = slice(c * BANK, (c + 1) * BANK)
+            w_cols = slice(g * N + b * P, g * N + (b + 1) * P)
+            nc.tensor.matmul_mx(
+                bank[:], lhsT=w3_w[:, w_cols].bitcast(FP8X4), lhsT_scale=w3_s[:, w_cols],
+                rhs=codes[g][:, cols].bitcast(FP8X4), rhs_scale=scales[g][:, cols],
+                start=(g == 0), stop=(g == GROUPS - 1),
+            )
+            return bank
+
+        def readout_close(c):
+            cols = slice(c * BANK, (c + 1) * BANK)
+            for b in range(NBLOCKS):
+                bank = readout_pass(1, c, b)
+                nc.vector.tensor_tensor(vis_sb[b][:, cols], bank[:], vis_sb[b][:, cols], MULT)
+                nc.sync.dma_start(out_0[b * P:(b + 1) * P, cols], vis_sb[b][:, cols])
+
+        def readout_open(c):
+            for b in range(NBLOCKS):
+                readout_pass(0, c, b)
+
+        s_copy = nc.scalar.copy
+        v_copy = nc.vector.tensor_copy
+
+        def next_tile(s, last_squares=None):
+            for half in range(2):
+                pair = [take("work", work_banks), take("work", work_banks)]
+                magnitudes(s, half * BANK, (half + 1) * BANK, pair, take("sum", sum_banks), last_squares if half else None)
+
+        def turn_tile(s):
+            for c in range(CHUNKS):
+                turn(s, c, s_copy)
+
+        magnitudes(0, 0, 256, [banks[0]], banks[2])
+        scatter(0, 0, 256)
+        magnitudes(0, 256, 512, [banks[1]], banks[3])
+        scatter(0, 256, 512)
+        magnitudes(0, 512, 1024, [banks[2], banks[0]], banks[1], w2_bf[1][:].bitcast(F32))
+        scatter(0, 512, 1024)
+        store_page(0)
+        quantize_w2(1)
+        next_tile(1, w2_bf[2][:].bitcast(F32))
+        for s in range(1, TILES):
+            scatter(s, 0, S)
+            store_page(s)
+            if s in (1, 3):
+                quantize_w2((s + 3) // 2)
+            if s + 1 < TILES:
+                next_tile(s + 1, w2_bf[3][:].bitcast(F32) if s == 2 else None)
+            if s <= 4:
+                turn_tile(s - 1)
+            if s == 4:
+                turn_back(0, 0, (s_copy, s_copy))
+            if s == 5:
+                for c in range(1, CHUNKS):
+                    turn_back(0, c, (s_copy, s_copy))
+                store_codes(0, 0, CHUNKS)
+                store_scales(0)
+            if s == 6:
+                turn_tile(4)
+        turn_tile(5)
+        turn_tile(6)
+        readout_open(0)
+
+        last = TILES - 1
+        turn(last, 0, s_copy)
+        turn(last, 1, v_copy)
+        turn_back(1, 0, (s_copy, v_copy))
+        store_codes(1, 0, 1)
+        turn(last, 2, s_copy)
+        turn(last, 3, s_copy)
+        readout_open(1)
+        for c in range(CHUNKS):
+            if c + 1 < CHUNKS:
+                turn_back(1, c + 1, (s_copy, s_copy))
+                store_codes(1, c + 1, c + 2)
+            if c + 2 == CHUNKS:
+                store_scales(1)
+            readout_close(c)
+            if c + 2 < CHUNKS:
+                readout_open(c + 2)

@@ -139,40 +139,38 @@ def tile_list_floorplan_beacon_tiles_kernel(
             nc.vector.tensor_copy(v_w[half][:], tab_w[:].bitcast(U32).indirect(entries))
             nc.vector.tensor_copy(v_s[half][:], tab_s[:].indirect(entries))
 
-        ring = {"work": 2, "sum": 0, "square": 0, "grouped": 0}
+        ring = {"turn": 0, "square": 0, "grouped": 0}
 
         def take(kind, items):
             item = items[ring[kind] % len(items)]
             ring[kind] = ring[kind] + 1
             return item
 
-        work_banks = [banks[0], banks[1], banks[2]]
-        sum_banks = [banks[3], banks[4], banks[7]]
+        product_banks = banks[0:4]
+        turn_banks = banks[4:8]
 
-        def magnitudes(s, j_from, j_to, product_banks, total, last_squares=None):
+        def products(s, q, bank, sq=None):
             r_cols = slice(s * P, (s + 1) * P)
-            made = []
-            for j0, bank in zip(range(j_from, j_to, 2 * P), product_banks):
-                for i in range(2):
-                    j = j0 + i * P
-                    words = v_w[j // BANK][:, j % BANK:j % BANK + P].bitcast(FP8X4)
-                    plane = v_s[j // BANK][:, j % BANK:j % BANK + P]
-                    nc.tensor.matmul_mx(
-                        bank[:, (2 * i) * P:(2 * i + 1) * P], lhsT=words, lhsT_scale=plane,
-                        rhs=w1_w[:, 2 * s * P:2 * (s + 1) * P].bitcast(FP4X4), rhs_scale=w1_s[:, r_cols],
-                        start=True, stop=True,
-                    )
-                    nc.tensor.matmul_mx(
-                        bank[:, (2 * i + 1) * P:(2 * i + 2) * P], lhsT=words, lhsT_scale=plane,
-                        rhs=w2_w[:, r_cols].bitcast(FP8X4), rhs_scale=w2_s[:, r_cols],
-                        start=True, stop=True,
-                    )
-                if last_squares is not None and j0 + 2 * P == j_to:
-                    sq = last_squares
-                else:
-                    sq = take("square", squares)[:]
-                nc.scalar.activation(sq, bank[:], SQUARE)
-                made.append(sq)
+            for i in range(2):
+                j = (2 * q + i) * P
+                words = v_w[j // BANK][:, j % BANK:j % BANK + P].bitcast(FP8X4)
+                plane = v_s[j // BANK][:, j % BANK:j % BANK + P]
+                nc.tensor.matmul_mx(
+                    bank[:, (2 * i) * P:(2 * i + 1) * P], lhsT=words, lhsT_scale=plane,
+                    rhs=w1_w[:, 2 * s * P:2 * (s + 1) * P].bitcast(FP4X4), rhs_scale=w1_s[:, r_cols],
+                    start=True, stop=True,
+                )
+                nc.tensor.matmul_mx(
+                    bank[:, (2 * i + 1) * P:(2 * i + 2) * P], lhsT=words, lhsT_scale=plane,
+                    rhs=w2_w[:, r_cols].bitcast(FP8X4), rhs_scale=w2_s[:, r_cols],
+                    start=True, stop=True,
+                )
+            if sq is None:
+                sq = take("square", squares)[:]
+            nc.scalar.activation(sq, bank[:], SQUARE)
+            return sq
+
+        def root(s, q_from, made, total):
             for n, sq in enumerate(made):
                 for i in range(2):
                     dst = total[:, (2 * n + i) * P:(2 * n + i + 1) * P]
@@ -181,7 +179,9 @@ def tile_list_floorplan_beacon_tiles_kernel(
                             dst, lhsT=sq[:, (2 * i + part) * P:(2 * i + part + 1) * P], rhs=ident[:],
                             start=(part == 0), stop=(part == 1), is_transpose=True,
                         )
-            nc.scalar.activation(hs[s % 2][:, j_from:j_to], total[:, 0:j_to - j_from], SQRT, bias=c0_cols[:, s:s + 1])
+            width = 2 * P * len(made)
+            j0 = 2 * P * q_from
+            nc.scalar.activation(hs[s % 2][:, j0:j0 + width], total[:, 0:width], SQRT, bias=c0_cols[:, s:s + 1])
 
         def scatter(s, j_from, j_to):
             nc.vector.tensor_tensor(
@@ -193,7 +193,7 @@ def tile_list_floorplan_beacon_tiles_kernel(
             nc.sync.dma_start(out_1[s * P:(s + 1) * P, :], pages[s][:])
 
         def turn(s, c, copy):
-            bank = take("work", work_banks)
+            bank = take("turn", turn_banks)
             for mb in range(4):
                 m0 = c * BANK + mb * P
                 nc.tensor.transpose(bank[:, mb * P:(mb + 1) * P], pages[s][:, m0:m0 + P], ident[:])
@@ -207,7 +207,7 @@ def tile_list_floorplan_beacon_tiles_kernel(
             ready = take("grouped", grouped)
             words = turned[c][:].bitcast(F32)
             for half in range(2):
-                bank = banks[5 + half]
+                bank = take("turn", turn_banks)
                 for i in range(4):
                     w0 = (4 * half + i) * P
                     nc.tensor.transpose(bank[:, i * P:(i + 1) * P], words[:, w0:w0 + P], ident[:])
@@ -229,7 +229,7 @@ def tile_list_floorplan_beacon_tiles_kernel(
                 nc.sync.dma_start(out_3[g, r:16:4, :].bitcast(I32), scales[g][r:P:32, :].bitcast(I32))
 
         def readout_pass(g, c, b):
-            bank = (sum_banks if c % 2 == 0 else work_banks)[b]
+            bank = product_banks[(c * NBLOCKS + b) % 4]
             cols = slice(c * BANK, (c + 1) * BANK)
             w_cols = slice(g * N + b * P, g * N + (b + 1) * P)
             nc.tensor.matmul_mx(
@@ -239,45 +239,52 @@ def tile_list_floorplan_beacon_tiles_kernel(
             )
             return bank
 
-        def readout_close(c):
+        def readout_close(c, b):
             cols = slice(c * BANK, (c + 1) * BANK)
-            for b in range(NBLOCKS):
-                bank = readout_pass(1, c, b)
-                nc.vector.tensor_tensor(vis_sb[b][:, cols], bank[:], vis_sb[b][:, cols], MULT)
-                nc.sync.dma_start(out_0[b * P:(b + 1) * P, cols], vis_sb[b][:, cols])
-
-        def readout_open(c):
-            for b in range(NBLOCKS):
-                readout_pass(0, c, b)
+            bank = readout_pass(1, c, b)
+            nc.vector.tensor_tensor(vis_sb[b][:, cols], bank[:], vis_sb[b][:, cols], MULT)
+            nc.sync.dma_start(out_0[b * P:(b + 1) * P, cols], vis_sb[b][:, cols])
 
         s_copy = nc.scalar.copy
         v_copy = nc.vector.tensor_copy
 
-        def next_tile(s, last_squares=None):
-            for half in range(2):
-                pair = [take("work", work_banks), take("work", work_banks)]
-                magnitudes(s, half * BANK, (half + 1) * BANK, pair, take("sum", sum_banks), last_squares if half else None)
+        def next_tile(s, first, second, sums, last_squares=None):
+            made = [products(s, 0, first[0]), products(s, 1, first[1])]
+            made = made + [products(s, 2, second[0]), products(s, 3, second[1], last_squares)]
+            root(s, 0, made[0:2], sums[0])
+            root(s, 2, made[2:4], sums[1])
 
         def turn_tile(s):
             for c in range(CHUNKS):
                 turn(s, c, s_copy)
 
-        magnitudes(0, 0, 256, [banks[0]], banks[2])
+        root(0, 0, [products(0, 0, banks[0])], banks[2])
         scatter(0, 0, 256)
-        magnitudes(0, 256, 512, [banks[1]], banks[3])
+        root(0, 1, [products(0, 1, banks[1])], banks[3])
         scatter(0, 256, 512)
-        magnitudes(0, 512, 1024, [banks[2], banks[0]], banks[1], w2_bf[1][:].bitcast(F32))
-        scatter(0, 512, 1024)
-        store_page(0)
+        root(0, 2, [products(0, 2, banks[2], w2_bf[1][:].bitcast(F32))], banks[5])
+        scatter(0, 512, 768)
+        late = products(0, 3, banks[0])
+        early = [products(1, 0, banks[1]), products(1, 1, banks[3])]
         quantize_w2(1)
-        next_tile(1, w2_bf[2][:].bitcast(F32))
-        for s in range(1, TILES):
-            scatter(s, 0, S)
-            store_page(s)
+        root(0, 3, [late], banks[7])
+        scatter(0, 768, 1024)
+        store_page(0)
+        root(1, 0, early, banks[4])
+        scatter(1, 0, 512)
+        root(1, 2, [products(1, 2, banks[5]), products(1, 3, banks[7], w2_bf[2][:].bitcast(F32))], banks[6])
+        scatter(1, 512, 1024)
+        store_page(1)
+        last = TILES - 1
+        pairs = (product_banks[0:2], product_banks[2:4])
+        for s in range(1, last):
+            if s > 1:
+                scatter(s, 0, S)
+                store_page(s)
             if s in (1, 3):
                 quantize_w2((s + 3) // 2)
-            if s + 1 < TILES:
-                next_tile(s + 1, w2_bf[3][:].bitcast(F32) if s == 2 else None)
+            first, second = pairs[(s + 1) % 2], pairs[s % 2]
+            next_tile(s + 1, first, second, first, w2_bf[3][:].bitcast(F32) if s == 2 else None)
             if s <= 4:
                 turn_tile(s - 1)
             if s == 4:
@@ -289,24 +296,26 @@ def tile_list_floorplan_beacon_tiles_kernel(
                 store_scales(0)
             if s == 6:
                 turn_tile(4)
+        scatter(last, 0, S)
+        store_page(last)
         turn_tile(5)
         turn_tile(6)
-        readout_open(0)
+        blocks = [(c, b) for c in range(CHUNKS) for b in range(NBLOCKS)]
+        for c, b in blocks[0:4]:
+            readout_pass(0, c, b)
 
-        last = TILES - 1
         turn(last, 0, s_copy)
         turn(last, 1, v_copy)
-        turn_back(1, 0, (s_copy, v_copy))
-        store_codes(1, 0, 1)
         turn(last, 2, s_copy)
         turn(last, 3, s_copy)
-        readout_open(1)
-        for c in range(CHUNKS):
-            if c + 1 < CHUNKS:
+        turn_back(1, 0, (s_copy, v_copy))
+        store_codes(1, 0, 1)
+        for n, (c, b) in enumerate(blocks):
+            if b == 0 and c + 1 < CHUNKS:
                 turn_back(1, c + 1, (s_copy, s_copy))
                 store_codes(1, c + 1, c + 2)
-            if c + 2 == CHUNKS:
-                store_scales(1)
-            readout_close(c)
-            if c + 2 < CHUNKS:
-                readout_open(c + 2)
+                if c + 2 == CHUNKS:
+                    store_scales(1)
+            readout_close(c, b)
+            if n + 4 < len(blocks):
+                readout_pass(0, *blocks[n + 4])

@@ -24,7 +24,8 @@ TILES = H // P
 GROUPS = H // 512
 CHUNKS = T2 // BANK
 NBLOCKS = N // P
-W2_PIECES = ((0, 256), (256, 512), (512, 768), (768, 1024))
+SLOT = {4: 0, 5: 2, 6: 1, 7: 3}
+W2_PIECES = ((0, 128), (128, 512), (512, 768), (768, 1024))
 
 
 def tile_list_floorplan_beacon_tiles_kernel(
@@ -44,100 +45,141 @@ def tile_list_floorplan_beacon_tiles_kernel(
         place = lists.tile([P, S // 16], U16, name="place")
         banks = [ps.tile([P, BANK], F32, name="bank" + str(i)) for i in range(8)]
 
-        tab_w = sb.tile([P, T], I32, name="tab_w", align_bytes=64)
-        tab_s = sb.tile([P, T], U8, name="tab_s", align_bytes=64)
+        tab_w = sb.tile([P, T], I32, name="tab_w", tag="table words", align_bytes=64)
+        tab_s = sb.tile([P, T], U8, name="tab_s", tag="table scales", align_bytes=64)
         v_w = tiles("v_w", 2, [P, S // 2], U32)
         v_s = tiles("v_s", 2, [P, S // 2], U8)
         w1_w = sb.tile([P, 2 * H], U8, name="w1_w", align_bytes=64)
         w1_s = sb.tile([P, H], U8, name="w1_s", align_bytes=64)
-        w2_raw = [sb.tile([P, 4, b - a], F32, name="w2_raw" + str(a), align_bytes=64) for a, b in W2_PIECES]
-        w2_bf = tiles("w2_bf", len(W2_PIECES), [P, 2 * BANK], BF16)
-        w2_w = sb.tile([P, H], U32, name="w2_w", align_bytes=64)
+        w1_s_dealt = sb.tile([P, BANK], U8, name="w1_s_dealt", align_bytes=64)
+        stage = tiles("stage", CHUNKS, [P, 2 * BANK], F32)
+        w2_rest = sb.tile([P, 3 * BANK], F32, name="w2_rest", tag="codes 1", align_bytes=64)
+        w2_raw = [stage[0][:, 0:BANK], w2_rest[:], stage[2][:], stage[3][:]]
+        w1_dealt = sb.tile([P, H], U8, name="w1_dealt", align_bytes=64)[:]
+        w2_dealt = sb.tile([P, 4 * BANK], BF16, name="w2_dealt", tag="third", align_bytes=64)
+        wgs_dealt = sb.tile([P, 4 * S], F32, name="wgs_dealt", align_bytes=64)
+        c0_dealt = sb.tile([P, 4], F32, name="c0_dealt", align_bytes=64)
+        w2_w = {0: sb.tile([P, P], U32, name="w2_w0", align_bytes=64)[:]}
         w2_s = sb.tile([P, H], U8, name="w2_s", align_bytes=64)
         w3_w = sb.tile([P, GROUPS * N], I32, name="w3_w", align_bytes=64)
         w3_s = sb.tile([P, GROUPS * N], U8, name="w3_s", align_bytes=64)
         c0_rows = sb.tile([P, P], F32, name="c0_rows", align_bytes=64)
-        c0_cols = sb.tile([P, TILES], F32, name="c0_cols", align_bytes=64)
+        c0_cols = sb.tile([P, 4], F32, name="c0_cols", align_bytes=64)
         ident = sb.tile([P, P], F32, name="ident", align_bytes=64)
         warm = tiles("warm", 2, [P, 1], F32)
         wgs_sb = sb.tile([P, S], F32, name="wgs_sb", align_bytes=64)
         pages = tiles("page", TILES, [P, T2], F32)
-        vis_sb = tiles("vis", NBLOCKS, [P, T2], F32)
+        vis_sb = tiles("vis", NBLOCKS - 1, [P, T2], F32)
         squares = tiles("squares", 4, [P, BANK], F32)
-        hs = tiles("h", 2, [P, S], F32)
         turned = tiles("turned", CHUNKS, [P, 4 * BANK], BF16)
-        grouped = tiles("grouped", 3, [P, 4 * BANK], BF16)
-        codes = tiles("codes", GROUPS, [P, T2], U32)
+        grouped = [tiles("grouped", CHUNKS, [P, 4 * BANK], BF16), turned]
+        w2_bf = [grouped[0][c][:, 0:2 * BANK] for c in range(3)]
+        later = {}
+        codes = [{}, {}]
+
+        def tenant(tag, name, shape, dtype):
+            return sb.tile(shape, dtype, name=name, tag=tag, align_bytes=64)[:]
         scales = tiles("scales", GROUPS, [P, T2], U8)
 
-        nc.vector.memset(tab_s[:].bitcast(I32), 0)
         nc.gpsimd.memset(w1_s[:].bitcast(I32), 0)
+        nc.vector.memset(tab_s[:].bitcast(I32), 0)
         nc.gpsimd.memset(c0_rows[:], 0.0)
         nc.vector.memset(warm[0][:], 1.0)
         nc.vector.memset(w3_s[:].bitcast(I32), 0)
-        make_identity(nc, ident[:])
-        nc.scalar.activation(warm[1][:], warm[0][:], SQRT)
 
         def load_w2(i):
             a, b = W2_PIECES[i]
-            nc.sync.dma_start(w2_raw[i][:], w2[:, a:b].rearrange("(p i) c -> p i c", i=4))
+            nc.sync.dma_start(w2_raw[i].rearrange("p (i c) -> p i c", i=4), w2[:, a:b].rearrange("(p i) c -> p i c", i=4))
 
-        def load_w1(half):
-            cols = slice(half * H // 4, (half + 1) * H // 4)
-            nc.sync.dma_start(w1_w[:].bitcast(I32)[:, cols], w1_words[0].bitcast(I32)[:, cols])
+        def rows_of(matrix, s):
+            if s < 4:
+                return matrix[s * P:(s + 1) * P, :]
+            return matrix[512:1024, :].rearrange("(p t) m -> t p m", t=4)[SLOT[s]]
 
         def load_page(s):
-            nc.sync.dma_start(pages[s][:], page0[s * P:(s + 1) * P, :])
+            nc.sync.dma_start(pages[s][:], rows_of(page0, s))
 
         nc.sync.dma_start(pick[:], offs)
-        nc.sync.dma_start(place[:], offs2)
-        load_w1(0)
+        landing = sb.tile([P, T // 4], I32, name="landing", tag="shared", align_bytes=64)
         for r in range(4):
-            nc.gpsimd.dma_start(tab_s[r:P:32, :].bitcast(I32), tab_scales[0, r:16:4, :].bitcast(I32))
+            nc.sync.dma_start(landing[r:P:32, :], tab_scales[0, r:16:4, :].bitcast(I32))
+        for quadrant in range(4):
+            rows = slice(32 * quadrant, 32 * quadrant + 4)
+            nc.vector.tensor_copy(tab_s[rows, :].bitcast(I32), landing[rows, :])
+        nc.gpsimd.dma_start(c0_rows[0:4, :], c0[0:512].rearrange("(s p) -> s p", p=P))
+        make_identity(nc, ident[:])
+        nc.scalar.activation(warm[1][:], warm[0][:], SQRT)
+        nc.sync.dma_start(w1_w[:].bitcast(I32), w1_words[0].bitcast(I32))
         load_w2(0)
         nc.sync.dma_start(tab_w[:], tab_words[0].rearrange("p t i -> p (t i)").bitcast(I32))
         for r in range(4):
-            nc.scalar.dma_start(w1_s[r:P:32, :].bitcast(I32), w1_scales[0, r:16:4, :].bitcast(I32))
-        nc.scalar.dma_start(c0_rows[0:TILES, :], c0.rearrange("(s p) -> s p", p=P))
-        nc.sync.dma_start(wgs_sb[:], wgs)
-        load_page(0)
+            nc.sync.dma_start(w1_s[r:P:32, :].bitcast(I32), w1_scales[0, r:16:4, :].bitcast(I32))
         load_w2(1)
+        nc.sync.dma_start(place[:], offs2)
+        nc.sync.dma_start(wgs_sb[:, 0:BANK], wgs[:, 0:BANK])
+        load_page(0)
+        nc.sync.dma_start(wgs_sb[:, BANK:S], wgs[:, BANK:S])
         load_page(1)
         load_w2(2)
-        load_w1(1)
-        load_page(2)
         load_w2(3)
-        for s in range(3, TILES):
+        load_page(2)
+        load_page(3)
+        nc.sync.dma_start(c0_dealt[:], c0[512:1024].rearrange("(p t) -> p t", t=4))
+        for s in range(4, TILES):
+            if s == 7:
+                nc.sync.dma_start(
+                    w3_w[:].rearrange("p (g n) -> p g n", g=GROUPS),
+                    w3_words.rearrange("g p n t -> p g (n t)").bitcast(I32),
+                )
+                for r in range(4):
+                    nc.sync.dma_start(
+                        w3_s[r:P:32, :].bitcast(I32).rearrange("q (g n) -> q g n", g=GROUPS),
+                        w3_scales.bitcast(I32)[:, r:16:4, :].rearrange("g q n -> q g n"),
+                    )
+                vis_sb.append(sb.tile([P, T2], F32, name="vis_last", tag="shared", align_bytes=64))
+                for b in range(NBLOCKS):
+                    nc.sync.dma_start(vis_sb[b][:], vis[b * P:(b + 1) * P, :])
+            t = SLOT[s]
+            for quadrant in (0, 2, 1, 3):
+                nc.sync.dma_start(
+                    wgs_dealt[32 * quadrant:32 * (quadrant + 1), t * S:(t + 1) * S],
+                    wgs.rearrange("(q t) j -> t q j", t=4)[t],
+                )
             load_page(s)
-        nc.sync.dma_start(
-            w3_w[:].rearrange("p (g n) -> p g n", g=GROUPS),
-            w3_words.rearrange("g p n t -> p g (n t)").bitcast(I32),
-        )
-        for r in range(4):
-            nc.sync.dma_start(
-                w3_s[r:P:32, :].bitcast(I32).rearrange("q (g n) -> q g n", g=GROUPS),
-                w3_scales.bitcast(I32)[:, r:16:4, :].rearrange("g q n -> q g n"),
-            )
-        for b in range(NBLOCKS):
-            nc.sync.dma_start(vis_sb[b][:], vis[b * P:(b + 1) * P, :])
 
         nc.tensor.transpose(banks[7][:, 0:P], c0_rows[:], ident[:])
-        nc.scalar.copy(c0_cols[:], banks[7][:, 0:TILES])
+        nc.scalar.copy(c0_cols[:], banks[7][:, 0:4])
 
-        def quantize_w2(i):
-            a, b = W2_PIECES[i]
+        nc.vector.tensor_copy(
+            w1_s_dealt[:].rearrange("p (t q) -> p t q", t=4),
+            w1_s[:, BANK:H].rearrange("p (q t) -> p t q", t=4),
+        )
+
+        def quantize_w2(i, piece, a, b, copy):
+            start = W2_PIECES[piece][0]
             rounded = w2_bf[i][:, 0:4 * (b - a)]
-            nc.scalar.copy(
-                rounded.rearrange("p (c i t) -> p c t i", i=4, t=4),
-                w2_raw[i][:].rearrange("p t (c i) -> p c t i", i=4),
-            )
-            nc.vector.quantize_mx(w2_w[:, a:b].bitcast(FP8X4), w2_s[:, a:b], rounded)
+            raw = w2_raw[piece].rearrange("p (t c) -> p t c", t=4)[:, :, a - start:b - start]
+            copy(rounded.rearrange("p (c i t) -> p c t i", i=4, t=4), raw.rearrange("p t (c i) -> p c t i", i=4))
+            if i > 0:
+                w2_w[i] = tenant("w2 codes " + str(i), "w2_w" + str(i), [P, b - a], U32)
+            nc.vector.quantize_mx(w2_w[i].bitcast(FP8X4), w2_s[:, a:b], rounded)
 
-        quantize_w2(0)
+        def deal_w2(i):
+            q0 = 64 * (i - 2)
+            nc.scalar.copy(
+                w2_dealt[:].rearrange("p (t q i) -> p q i t", t=4, i=4)[:, q0:q0 + 64],
+                w2_raw[i].rearrange("p (i q t) -> p q i t", i=4, t=4),
+            )
+
+        quantize_w2(0, 0, 0, P, nc.scalar.copy)
         for half in range(2):
-            entries = pick[:, 32 * half:32 * (half + 1)]
-            nc.vector.tensor_copy(v_w[half][:], tab_w[:].bitcast(U32).indirect(entries))
-            nc.vector.tensor_copy(v_s[half][:], tab_s[:].indirect(entries))
+            nc.vector.tensor_copy(v_s[half][:], tab_s[:].indirect(pick[:, 32 * half:32 * (half + 1)]))
+        for half in range(2):
+            nc.vector.tensor_copy(v_w[half][:], tab_w[:].bitcast(U32).indirect(pick[:, 32 * half:32 * (half + 1)]))
+        nc.vector.tensor_copy(
+            w1_dealt.rearrange("p (t q b) -> p t q b", t=4, b=2),
+            w1_w[:, H:2 * H].rearrange("p (q t b) -> p t q b", t=4, b=2),
+        )
 
         ring = {"turn": 0, "square": 0, "grouped": 0}
 
@@ -147,22 +189,39 @@ def tile_list_floorplan_beacon_tiles_kernel(
             return item
 
         product_banks = banks[0:4]
-        turn_banks = banks[4:8]
+        sum_banks = (banks[4:6], banks[6:8])
+
+        quantize_w2(1, 1, P, 2 * P, nc.vector.tensor_copy)
+        quantize_w2(2, 1, 2 * P, 4 * P, nc.vector.tensor_copy)
+        even, odd = (tenant("roots" + str(i), "h" + str(i), [P, S], F32) for i in range(2))
+        h_of = [None, tenant("roots of tile 1", "h_1", [P, S], F32), even, odd, even, odd, even, odd]
+        quarters = [tenant("quarter" + str(n), "h0_" + str(n), [P, 2 * P], F32) for n in range(4)]
+
+        def roots_of(s, j_from, j_to):
+            return quarters[j_from // (2 * P)] if s == 0 else h_of[s][:, j_from:j_to]
 
         def products(s, q, bank, sq=None):
-            r_cols = slice(s * P, (s + 1) * P)
+            if s < 4:
+                r_cols = slice(s * P, (s + 1) * P)
+                w1_codes, w1_plane = w1_w[:, 2 * s * P:2 * (s + 1) * P], w1_s[:, r_cols]
+                w2_codes = w2_w[s] if s < 2 else w2_w[2][:, (s - 2) * P:(s - 1) * P]
+            else:
+                t = SLOT[s]
+                r_cols = slice(BANK + t * P, BANK + (t + 1) * P)
+                w1_codes, w1_plane = w1_dealt[:, 2 * t * P:2 * (t + 1) * P], w1_s_dealt[:, t * P:(t + 1) * P]
+                w2_codes = later["w2"][:, t * P:(t + 1) * P]
             for i in range(2):
                 j = (2 * q + i) * P
                 words = v_w[j // BANK][:, j % BANK:j % BANK + P].bitcast(FP8X4)
                 plane = v_s[j // BANK][:, j % BANK:j % BANK + P]
                 nc.tensor.matmul_mx(
                     bank[:, (2 * i) * P:(2 * i + 1) * P], lhsT=words, lhsT_scale=plane,
-                    rhs=w1_w[:, 2 * s * P:2 * (s + 1) * P].bitcast(FP4X4), rhs_scale=w1_s[:, r_cols],
+                    rhs=w1_codes.bitcast(FP4X4), rhs_scale=w1_plane,
                     start=True, stop=True,
                 )
                 nc.tensor.matmul_mx(
                     bank[:, (2 * i + 1) * P:(2 * i + 2) * P], lhsT=words, lhsT_scale=plane,
-                    rhs=w2_w[:, r_cols].bitcast(FP8X4), rhs_scale=w2_s[:, r_cols],
+                    rhs=w2_codes.bitcast(FP8X4), rhs_scale=w2_s[:, r_cols],
                     start=True, stop=True,
                 )
             if sq is None:
@@ -170,7 +229,7 @@ def tile_list_floorplan_beacon_tiles_kernel(
             nc.scalar.activation(sq, bank[:], SQUARE)
             return sq
 
-        def root(s, q_from, made, total):
+        def add_squares(made, total):
             for n, sq in enumerate(made):
                 for i in range(2):
                     dst = total[:, (2 * n + i) * P:(2 * n + i + 1) * P]
@@ -179,21 +238,22 @@ def tile_list_floorplan_beacon_tiles_kernel(
                             dst, lhsT=sq[:, (2 * i + part) * P:(2 * i + part + 1) * P], rhs=ident[:],
                             start=(part == 0), stop=(part == 1), is_transpose=True,
                         )
-            width = 2 * P * len(made)
-            j0 = 2 * P * q_from
-            nc.scalar.activation(hs[s % 2][:, j0:j0 + width], total[:, 0:width], SQRT, bias=c0_cols[:, s:s + 1])
+
+        def root(s, j0, width, total):
+            bias = c0_cols[:, s:s + 1] if s < 4 else c0_dealt[:, SLOT[s]:SLOT[s] + 1]
+            nc.scalar.activation(roots_of(s, j0, j0 + width), total[:, 0:width], SQRT, bias=bias)
 
         def scatter(s, j_from, j_to):
+            factor = wgs_sb[:] if s < 4 else wgs_dealt[:, SLOT[s] * S:(SLOT[s] + 1) * S]
             nc.vector.tensor_tensor(
                 pages[s][:].indirect(place[:, j_from // 16:j_to // 16]),
-                hs[s % 2][:, j_from:j_to], wgs_sb[:, j_from:j_to], MULT,
+                roots_of(s, j_from, j_to), factor[:, j_from:j_to], MULT,
             )
 
         def store_page(s):
-            nc.sync.dma_start(out_1[s * P:(s + 1) * P, :], pages[s][:])
+            nc.sync.dma_start(rows_of(out_1, s), pages[s][:])
 
-        def turn(s, c, copy):
-            bank = take("turn", turn_banks)
+        def turn(s, c, copy, bank):
             for mb in range(4):
                 m0 = c * BANK + mb * P
                 nc.tensor.transpose(bank[:, mb * P:(mb + 1) * P], pages[s][:, m0:m0 + P], ident[:])
@@ -203,11 +263,11 @@ def tile_list_floorplan_beacon_tiles_kernel(
                 bank[:].rearrange("m (b q u e) -> m b u q e", b=4, u=2, e=2),
             )
 
-        def turn_back(g, c, copies):
-            ready = take("grouped", grouped)
+        def turn_back(c, copies, into):
+            ready = grouped[0][c]
             words = turned[c][:].bitcast(F32)
             for half in range(2):
-                bank = take("turn", turn_banks)
+                bank = into[half]
                 for i in range(4):
                     w0 = (4 * half + i) * P
                     nc.tensor.transpose(bank[:, i * P:(i + 1) * P], words[:, w0:w0 + P], ident[:])
@@ -215,107 +275,147 @@ def tile_list_floorplan_beacon_tiles_kernel(
                     ready[:].bitcast(F32)[:, half * BANK:(half + 1) * BANK].rearrange("p (b m u) -> p b m u", b=2, u=2),
                     bank[:].rearrange("p (b u m) -> p b m u", b=2, u=2),
                 )
+
+        def round_into_pairs(s, c):
+            u, e = divmod(SLOT[s], 2)
+            pairs = stage[c][:].bitcast(BF16).rearrange("p (u m e) -> p u m e", u=2, e=2)
+            nc.scalar.copy(pairs[:, u, :, e], pages[s][:, c * BANK:(c + 1) * BANK])
+
+        def join_pairs(c):
+            copy, word = (nc.vector.tensor_copy, I32) if c == 0 else (nc.scalar.copy, U32)
+            copy(
+                grouped[1][c][:].bitcast(word).rearrange("p (m u) -> p m u", u=2),
+                stage[c][:].bitcast(word).rearrange("p (u m) -> p m u", u=2),
+            )
+
+        def quantize_page(g, c):
             cols = slice(c * BANK, (c + 1) * BANK)
-            nc.vector.quantize_mx(codes[g][:, cols].bitcast(FP8X4), scales[g][:, cols], ready[:])
+            ready = grouped[g][c]
+            nc.vector.quantize_mx(codes[g][c].bitcast(FP8X4), scales[g][:, cols], ready[:])
 
         def store_codes(g, c_from, c_to):
             cols = slice(c_from * BANK, c_to * BANK)
+            within = slice((c_from % 2) * BANK, (c_from % 2 + c_to - c_from) * BANK)
             nc.sync.dma_start(
-                out_2[g].rearrange("p m t -> p (m t)").bitcast(I32)[:, cols], codes[g][:, cols].bitcast(I32)
+                out_2[g].rearrange("p m t -> p (m t)").bitcast(I32)[:, cols], code_pairs[g][c_from // 2][:, within].bitcast(I32)
             )
 
         def store_scales(g):
             for r in range(4):
                 nc.sync.dma_start(out_3[g, r:16:4, :].bitcast(I32), scales[g][r:P:32, :].bitcast(I32))
 
-        def readout_pass(g, c, b):
-            bank = product_banks[(c * NBLOCKS + b) % 4]
+        def readout_pass(g, c, b, bank):
             cols = slice(c * BANK, (c + 1) * BANK)
             w_cols = slice(g * N + b * P, g * N + (b + 1) * P)
             nc.tensor.matmul_mx(
                 bank[:], lhsT=w3_w[:, w_cols].bitcast(FP8X4), lhsT_scale=w3_s[:, w_cols],
-                rhs=codes[g][:, cols].bitcast(FP8X4), rhs_scale=scales[g][:, cols],
+                rhs=codes[g][c].bitcast(FP8X4), rhs_scale=scales[g][:, cols],
                 start=(g == 0), stop=(g == GROUPS - 1),
             )
-            return bank
 
-        def readout_close(c, b):
+        def readout_close(c, b, bank):
             cols = slice(c * BANK, (c + 1) * BANK)
-            bank = readout_pass(1, c, b)
+            readout_pass(1, c, b, bank)
             nc.vector.tensor_tensor(vis_sb[b][:, cols], bank[:], vis_sb[b][:, cols], MULT)
-            nc.sync.dma_start(out_0[b * P:(b + 1) * P, cols], vis_sb[b][:, cols])
+
 
         s_copy = nc.scalar.copy
         v_copy = nc.vector.tensor_copy
 
-        def next_tile(s, first, second, sums, last_squares=None):
-            made = [products(s, 0, first[0]), products(s, 1, first[1])]
-            made = made + [products(s, 2, second[0]), products(s, 3, second[1], last_squares)]
-            root(s, 0, made[0:2], sums[0])
-            root(s, 2, made[2:4], sums[1])
+        def all_products(s, held=(None, None, None, None)):
+            return [products(s, n, product_banks[n], held[n]) for n in range(4)]
+
+        def all_sums(s, made):
+            for half in range(2):
+                add_squares(made[2 * half:2 * half + 2], sum_banks[s % 2][half])
+
+        def all_roots(s):
+            for half in range(2):
+                root(s, half * BANK, BANK, sum_banks[s % 2][half])
 
         def turn_tile(s):
             for c in range(CHUNKS):
-                turn(s, c, s_copy)
+                turn(s, c, s_copy, product_banks[c])
 
-        root(0, 0, [products(0, 0, banks[0])], banks[2])
-        scatter(0, 0, 256)
-        root(0, 1, [products(0, 1, banks[1])], banks[3])
-        scatter(0, 256, 512)
-        root(0, 2, [products(0, 2, banks[2], w2_bf[1][:].bitcast(F32))], banks[5])
-        scatter(0, 512, 768)
-        late = products(0, 3, banks[0])
-        early = [products(1, 0, banks[1]), products(1, 1, banks[3])]
-        quantize_w2(1)
-        root(0, 3, [late], banks[7])
-        scatter(0, 768, 1024)
+        def round_tile(s):
+            for c in range(CHUNKS):
+                round_into_pairs(s, c)
+
+        for n in range(4):
+            add_squares([products(0, n, banks[n])], banks[n + 2])
+            root(0, 256 * n, 256, banks[n + 2])
+            scatter(0, 256 * n, 256 * (n + 1))
         store_page(0)
-        root(1, 0, early, banks[4])
-        scatter(1, 0, 512)
-        root(1, 2, [products(1, 2, banks[5]), products(1, 3, banks[7], w2_bf[2][:].bitcast(F32))], banks[6])
-        scatter(1, 512, 1024)
-        store_page(1)
+        all_sums(1, all_products(1, (None, None, None, w2_dealt[:, 0:2 * BANK].bitcast(F32))))
+        all_roots(1)
+        deal_w2(2)
+        deal_w2(3)
+        all_sums(2, all_products(2))
         last = TILES - 1
-        pairs = (product_banks[0:2], product_banks[2:4])
-        for s in range(1, last):
-            if s > 1:
+        for s in range(1, TILES):
+            if s == 1:
+                scatter(s, 0, BANK)
+                scatter(s, BANK, S)
+            else:
                 scatter(s, 0, S)
-                store_page(s)
-            if s in (1, 3):
-                quantize_w2((s + 3) // 2)
-            first, second = pairs[(s + 1) % 2], pairs[s % 2]
-            next_tile(s + 1, first, second, first, w2_bf[3][:].bitcast(F32) if s == 2 else None)
+            store_page(s)
+            if s == 1:
+                later["w2"] = tenant("roots of tile 1", "w2_w_dealt", [P, BANK], U32)
+                nc.vector.quantize_mx(later["w2"].bitcast(FP8X4), w2_s[:, BANK:H], w2_dealt[:])
+            if s < last:
+                all_roots(s + 1)
+            made = None
+            if s in (4, 5):
+                made = all_products(s + 2, [stage[c][:, (s - 4) * BANK:(s - 3) * BANK] for c in range(CHUNKS)])
+            elif s < 4:
+                made = all_products(s + 2)
             if s <= 4:
                 turn_tile(s - 1)
+            if made is not None:
+                all_sums(s + 2, made)
             if s == 4:
-                turn_back(0, 0, (s_copy, s_copy))
-            if s == 5:
-                for c in range(1, CHUNKS):
-                    turn_back(0, c, (s_copy, s_copy))
-                store_codes(0, 0, CHUNKS)
-                store_scales(0)
+                turn_back(0, (s_copy, s_copy), product_banks[0:2])
             if s == 6:
-                turn_tile(4)
-        scatter(last, 0, S)
-        store_page(last)
-        turn_tile(5)
-        turn_tile(6)
-        blocks = [(c, b) for c in range(CHUNKS) for b in range(NBLOCKS)]
-        for c, b in blocks[0:4]:
-            readout_pass(0, c, b)
+                turn_back(1, (s_copy, s_copy), product_banks[0:2])
+                turn_back(2, (s_copy, s_copy), product_banks[2:4])
+            if s == last:
+                turn_back(3, (s_copy, s_copy), sum_banks[0])
+            if s >= 5:
+                round_tile(s - 1)
 
-        turn(last, 0, s_copy)
-        turn(last, 1, v_copy)
-        turn(last, 2, s_copy)
-        turn(last, 3, s_copy)
-        turn_back(1, 0, (s_copy, v_copy))
-        store_codes(1, 0, 1)
-        for n, (c, b) in enumerate(blocks):
-            if b == 0 and c + 1 < CHUNKS:
-                turn_back(1, c + 1, (s_copy, s_copy))
-                store_codes(1, c + 1, c + 2)
-                if c + 2 == CHUNKS:
-                    store_scales(1)
-            readout_close(c, b)
-            if n + 4 < len(blocks):
-                readout_pass(0, *blocks[n + 4])
+        codes_1 = tenant("codes 1", "codes_1", [P, T2], U32)
+        code_pairs = [
+            [tenant("roots" + str(pair), "codes_0" + str(pair), [P, 2 * BANK], U32) for pair in range(2)],
+            [codes_1[:, 0:2 * BANK], codes_1[:, 2 * BANK:4 * BANK]],
+        ]
+        for g in range(GROUPS):
+            for c in range(CHUNKS):
+                codes[g][c] = code_pairs[g][c // 2][:, (c % 2) * BANK:(c % 2 + 1) * BANK]
+
+        def finish(g, c):
+            quantize_page(g, c)
+            if g == 1:
+                store_codes(g, c, c + 1)
+            elif c % 2 == 1:
+                store_codes(g, c - 1, c + 1)
+            if c + 1 == CHUNKS:
+                store_scales(g)
+
+        def store_out(b, c_from, c_to):
+            cols = slice(c_from * BANK, c_to * BANK)
+            nc.sync.dma_start(out_0[b * P:(b + 1) * P, cols], vis_sb[b][:, cols])
+
+        for c in range(CHUNKS):
+            round_into_pairs(last, c)
+            join_pairs(c)
+        for c in range(CHUNKS):
+            finish(0, c)
+        finish(1, 0)
+        order = [(c, b) for c in range(CHUNKS) for b in range(NBLOCKS)]
+        for n, (c, b) in enumerate(order):
+            bank = banks[n % 8]
+            readout_pass(0, c, b, bank)
+            readout_close(c, b, bank)
+            store_out(b, c, c + 1)
+            if b == 1 and c + 1 < CHUNKS:
+                finish(1, c + 1)

@@ -116,8 +116,8 @@ def tile_list_floorplan_beacon_tiles_kernel(
             nc.sync.dma_start(w1_s[r:P:32, :].bitcast(I32), w1_scales[0, r:16:4, :].bitcast(I32))
         load_w2(1)
         nc.sync.dma_start(place[:], offs2)
-        nc.sync.dma_start(wgs_sb[:, 0:BANK], wgs[:, 0:BANK])
         load_page(0)
+        nc.sync.dma_start(wgs_sb[:, 0:BANK], wgs[:, 0:BANK])
         nc.sync.dma_start(wgs_sb[:, BANK:S], wgs[:, BANK:S])
         load_page(1)
         load_w2(2)
@@ -177,8 +177,8 @@ def tile_list_floorplan_beacon_tiles_kernel(
         for half in range(2):
             nc.vector.tensor_copy(v_w[half][:], tab_w[:].bitcast(U32).indirect(pick[:, 32 * half:32 * (half + 1)]))
         nc.vector.tensor_copy(
-            w1_dealt.rearrange("p (t q b) -> p t q b", t=4, b=2),
-            w1_w[:, H:2 * H].rearrange("p (q t b) -> p t q b", t=4, b=2),
+            w1_dealt.bitcast(U16).rearrange("p (t q) -> p t q", t=4),
+            w1_w[:, H:2 * H].bitcast(U16).rearrange("p (q t) -> p t q", t=4),
         )
 
         ring = {"turn": 0, "square": 0, "grouped": 0}
@@ -191,16 +191,16 @@ def tile_list_floorplan_beacon_tiles_kernel(
         product_banks = banks[0:4]
         sum_banks = (banks[4:6], banks[6:8])
 
-        quantize_w2(1, 1, P, 2 * P, nc.vector.tensor_copy)
+        quantize_w2(1, 1, P, 2 * P, nc.scalar.copy)
         quantize_w2(2, 1, 2 * P, 4 * P, nc.vector.tensor_copy)
+        h_0 = sb.tile([P, S], F32, name="h_0", align_bytes=64)[:]
         even, odd = (tenant("roots" + str(i), "h" + str(i), [P, S], F32) for i in range(2))
-        h_of = [None, tenant("roots of tile 1", "h_1", [P, S], F32), even, odd, even, odd, even, odd]
-        quarters = [tenant("quarter" + str(n), "h0_" + str(n), [P, 2 * P], F32) for n in range(4)]
+        h_of = [h_0, tenant("roots of tile 1", "h_1", [P, S], F32), even, odd, even, odd, even, odd]
 
         def roots_of(s, j_from, j_to):
-            return quarters[j_from // (2 * P)] if s == 0 else h_of[s][:, j_from:j_to]
+            return h_of[s][:, j_from:j_to]
 
-        def products(s, q, bank, sq=None):
+        def products(s, q, bank, sq=None, second_bank=None):
             if s < 4:
                 r_cols = slice(s * P, (s + 1) * P)
                 w1_codes, w1_plane = w1_w[:, 2 * s * P:2 * (s + 1) * P], w1_s[:, r_cols]
@@ -210,7 +210,12 @@ def tile_list_floorplan_beacon_tiles_kernel(
                 r_cols = slice(BANK + t * P, BANK + (t + 1) * P)
                 w1_codes, w1_plane = w1_dealt[:, 2 * t * P:2 * (t + 1) * P], w1_s_dealt[:, t * P:(t + 1) * P]
                 w2_codes = later["w2"][:, t * P:(t + 1) * P]
+            if sq is None:
+                sq = take("square", squares)[:]
             for i in range(2):
+                if i == 1 and second_bank is not None:
+                    nc.scalar.activation(sq[:, 0:2 * P], bank[:, 0:2 * P], SQUARE)
+                    bank = second_bank
                 j = (2 * q + i) * P
                 words = v_w[j // BANK][:, j % BANK:j % BANK + P].bitcast(FP8X4)
                 plane = v_s[j // BANK][:, j % BANK:j % BANK + P]
@@ -224,9 +229,8 @@ def tile_list_floorplan_beacon_tiles_kernel(
                     rhs=w2_codes.bitcast(FP8X4), rhs_scale=w2_s[:, r_cols],
                     start=True, stop=True,
                 )
-            if sq is None:
-                sq = take("square", squares)[:]
-            nc.scalar.activation(sq, bank[:], SQUARE)
+            first = 0 if second_bank is None else 2 * P
+            nc.scalar.activation(sq[:, first:BANK], bank[:, first:BANK], SQUARE)
             return sq
 
         def add_squares(made, total):
@@ -342,9 +346,10 @@ def tile_list_floorplan_beacon_tiles_kernel(
                 round_into_pairs(s, c)
 
         for n in range(4):
-            add_squares([products(0, n, banks[n])], banks[n + 2])
+            add_squares([products(0, n, banks[n], None, banks[6] if n == 0 else None)], banks[n + 2])
             root(0, 256 * n, 256, banks[n + 2])
-            scatter(0, 256 * n, 256 * (n + 1))
+            if n != 2:
+                scatter(0, 256 * min(n, 2), 256 * (n + 1))
         store_page(0)
         all_sums(1, all_products(1, (None, None, None, w2_dealt[:, 0:2 * BANK].bitcast(F32))))
         all_roots(1)

@@ -48,7 +48,7 @@ def tile_list_floorplan_beacon_tiles_kernel(
         tab_w = sb.tile([P, T], I32, name="tab_w", tag="table words", align_bytes=64)
         tab_s = sb.tile([P, T], U8, name="tab_s", tag="table scales", align_bytes=64)
         v_w = tiles("v_w", 2, [P, S // 2], U32)
-        v_s = tiles("v_s", 2, [P, S // 2], U8)
+        v_s = tiles("v_s", 1, [P, S // 2], U8)
         w1_w = sb.tile([P, 2 * H], U8, name="w1_w", align_bytes=64)
         w1_s = sb.tile([P, H], U8, name="w1_s", align_bytes=64)
         w1_s_dealt = sb.tile([P, BANK], U8, name="w1_s_dealt", align_bytes=64)
@@ -161,7 +161,7 @@ def tile_list_floorplan_beacon_tiles_kernel(
             raw = w2_raw[piece].rearrange("p (t c) -> p t c", t=4)[:, :, a - start:b - start]
             copy(rounded.rearrange("p (c i t) -> p c t i", i=4, t=4), raw.rearrange("p t (c i) -> p c t i", i=4))
             if i > 0:
-                w2_w[i] = tenant("w2 codes " + str(i), "w2_w" + str(i), [P, b - a], U32)
+                w2_w[i] = tenant("first roots" if i == 2 else "w2 codes", "w2_w" + str(i), [P, b - a], U32)
             nc.vector.quantize_mx(w2_w[i].bitcast(FP8X4), w2_s[:, a:b], rounded)
 
         def deal_w2(i):
@@ -172,10 +172,11 @@ def tile_list_floorplan_beacon_tiles_kernel(
             )
 
         quantize_w2(0, 0, 0, P, nc.scalar.copy)
-        for half in range(2):
-            nc.vector.tensor_copy(v_s[half][:], tab_s[:].indirect(pick[:, 32 * half:32 * (half + 1)]))
+        nc.vector.tensor_copy(v_s[0][:], tab_s[:].indirect(pick[:, 0:32]))
         for half in range(2):
             nc.vector.tensor_copy(v_w[half][:], tab_w[:].bitcast(U32).indirect(pick[:, 32 * half:32 * (half + 1)]))
+        v_s.append(tenant("table words", "v_s1", [P, S // 2], U8))
+        nc.vector.tensor_copy(v_s[1], tab_s[:].indirect(pick[:, 32:64]))
         nc.vector.tensor_copy(
             w1_dealt.bitcast(U16).rearrange("p (t q) -> p t q", t=4),
             w1_w[:, H:2 * H].bitcast(U16).rearrange("p (q t) -> p t q", t=4),
@@ -192,13 +193,13 @@ def tile_list_floorplan_beacon_tiles_kernel(
         sum_banks = (banks[4:6], banks[6:8])
 
         quantize_w2(1, 1, P, 2 * P, nc.scalar.copy)
-        quantize_w2(2, 1, 2 * P, 4 * P, nc.vector.tensor_copy)
+        h_first = tenant("first roots", "h_first", [P, 2 * P], F32)
         h_0 = sb.tile([P, S], F32, name="h_0", align_bytes=64)[:]
         even, odd = (tenant("roots" + str(i), "h" + str(i), [P, S], F32) for i in range(2))
         h_of = [h_0, tenant("roots of tile 1", "h_1", [P, S], F32), even, odd, even, odd, even, odd]
 
         def roots_of(s, j_from, j_to):
-            return h_of[s][:, j_from:j_to]
+            return h_first if (s, j_from) == (0, 0) else h_of[s][:, j_from:j_to]
 
         def products(s, q, bank, sq=None, second_bank=None):
             if s < 4:
@@ -346,10 +347,12 @@ def tile_list_floorplan_beacon_tiles_kernel(
                 round_into_pairs(s, c)
 
         for n in range(4):
-            add_squares([products(0, n, banks[n], None, banks[6] if n == 0 else None)], banks[n + 2])
+            add_squares([products(0, n, banks[n], w2_bf[2].bitcast(F32) if n == 1 else None, banks[6] if n == 0 else None)], banks[n + 2])
             root(0, 256 * n, 256, banks[n + 2])
             if n != 2:
                 scatter(0, 256 * min(n, 2), 256 * (n + 1))
+            if n == 1:
+                quantize_w2(2, 1, 2 * P, 4 * P, nc.scalar.copy)
         store_page(0)
         all_sums(1, all_products(1, (None, None, None, w2_dealt[:, 0:2 * BANK].bitcast(F32))))
         all_roots(1)

@@ -150,7 +150,7 @@ def tile_list_floorplan_beacon_tiles_kernel(
         nc.tensor.transpose(banks[7][:, 0:P], c0_rows[:], ident[:])
         nc.scalar.copy(c0_cols[:], banks[7][:, 0:4])
 
-        nc.vector.tensor_copy(
+        nc.gpsimd.tensor_copy(
             w1_s_dealt[:].rearrange("p (t q) -> p t q", t=4),
             w1_s[:, BANK:H].rearrange("p (q t) -> p t q", t=4),
         )

@@ -24,8 +24,10 @@ TILES = H // P
 GROUPS = H // 512
 CHUNKS = T2 // BANK
 NBLOCKS = N // P
+PLANE_ROW = (4, 0)
 SLOT = {4: 0, 5: 2, 6: 1, 7: 3}
-W2_PIECES = ((0, 128), (128, 512), (512, 768), (768, 1024))
+W2_PIECES = ((0, 128), (128, 256), (384, 512), (512, 768), (768, 1024), (256, 384))
+PICKS = ((0, 256), (256, 512), (512, 1024))
 
 
 def tile_list_floorplan_beacon_tiles_kernel(
@@ -47,15 +49,14 @@ def tile_list_floorplan_beacon_tiles_kernel(
 
         tab_w = sb.tile([P, T], I32, name="tab_w", tag="table words", align_bytes=64)
         tab_s = sb.tile([P, T], U8, name="tab_s", tag="table scales", align_bytes=64)
-        v_w = tiles("v_w", 2, [P, S // 2], U32)
-        v_s = tiles("v_s", 1, [P, S // 2], U8)
+        v_w = [sb.tile([P, b - a], U32, name="v_w" + str(a), align_bytes=64) for a, b in PICKS]
+        picked_s = sb.tile([P, S], U8, name="picked_s", align_bytes=64)
+        v_s = sb.tile([P, S], U8, name="v_s", align_bytes=64)
         w1_w = sb.tile([P, 2 * H], U8, name="w1_w", align_bytes=64)
         w1_s = sb.tile([P, H], U8, name="w1_s", align_bytes=64)
-        w1_s_dealt = sb.tile([P, BANK], U8, name="w1_s_dealt", align_bytes=64)
         stage = tiles("stage", CHUNKS, [P, 2 * BANK], F32)
-        w2_rest = sb.tile([P, 3 * BANK], F32, name="w2_rest", tag="codes 1", align_bytes=64)
-        w2_raw = [stage[0][:, 0:BANK], w2_rest[:], stage[2][:], stage[3][:]]
-        w1_dealt = sb.tile([P, H], U8, name="w1_dealt", align_bytes=64)[:]
+        w2_rest = sb.tile([P, BANK], F32, name="w2_rest", tag="codes 1", align_bytes=64)
+        w2_raw = [stage[0][:, 0:BANK], stage[0][:, 0:BANK], w2_rest[:], stage[2][:], stage[3][:], stage[1][:, 0:BANK]]
         w2_dealt = sb.tile([P, 4 * BANK], BF16, name="w2_dealt", tag="third", align_bytes=64)
         wgs_dealt = sb.tile([P, 4 * S], F32, name="wgs_dealt", align_bytes=64)
         c0_dealt = sb.tile([P, 4], F32, name="c0_dealt", align_bytes=64)
@@ -68,12 +69,12 @@ def tile_list_floorplan_beacon_tiles_kernel(
         ident = sb.tile([P, P], F32, name="ident", align_bytes=64)
         warm = tiles("warm", 2, [P, 1], F32)
         wgs_sb = sb.tile([P, S], F32, name="wgs_sb", align_bytes=64)
-        pages = tiles("page", TILES, [P, T2], F32)
+        pages = {s: sb.tile([P, T2], F32, name="page" + str(s), align_bytes=64) for s in range(1, TILES)}
         vis_sb = tiles("vis", NBLOCKS - 1, [P, T2], F32)
         squares = tiles("squares", 4, [P, BANK], F32)
         turned = tiles("turned", CHUNKS, [P, 4 * BANK], BF16)
         grouped = [tiles("grouped", CHUNKS, [P, 4 * BANK], BF16), turned]
-        w2_bf = [grouped[0][c][:, 0:2 * BANK] for c in range(3)]
+        w2_bf = [grouped[0][c][:, 0:2 * BANK] for c in range(4)]
         later = {}
         codes = [{}, {}]
 
@@ -86,10 +87,20 @@ def tile_list_floorplan_beacon_tiles_kernel(
         nc.gpsimd.memset(c0_rows[:], 0.0)
         nc.vector.memset(warm[0][:], 1.0)
         nc.vector.memset(w3_s[:].bitcast(I32), 0)
+        nc.vector.memset(v_s[:].bitcast(I32), 0)
 
         def load_w2(i):
             a, b = W2_PIECES[i]
             nc.sync.dma_start(w2_raw[i].rearrange("p (i c) -> p i c", i=4), w2[:, a:b].rearrange("(p i) c -> p i c", i=4))
+
+        def quantize_w2(i, piece, a, b, copy):
+            start = W2_PIECES[piece][0]
+            rounded = w2_bf[i][:, 0:4 * (b - a)]
+            raw = w2_raw[piece].rearrange("p (t c) -> p t c", t=4)[:, :, a - start:b - start]
+            copy(rounded.rearrange("p (c i t) -> p c t i", i=4, t=4), raw.rearrange("p t (c i) -> p c t i", i=4))
+            if i > 0:
+                w2_w[i] = tenant("first roots1" if i == 2 else "w2 codes" + str(i), "w2_w" + str(i), [P, b - a], U32)
+            nc.vector.quantize_mx(w2_w[i].bitcast(FP8X4), w2_s[:, a:b], rounded)
 
         def rows_of(matrix, s):
             if s < 4:
@@ -99,29 +110,36 @@ def tile_list_floorplan_beacon_tiles_kernel(
         def load_page(s):
             nc.sync.dma_start(pages[s][:], rows_of(page0, s))
 
-        nc.sync.dma_start(pick[:], offs)
         landing = sb.tile([P, T // 4], I32, name="landing", tag="shared", align_bytes=64)
-        for r in range(4):
-            nc.sync.dma_start(landing[r:P:32, :], tab_scales[0, r:16:4, :].bitcast(I32))
-        for quadrant in range(4):
-            rows = slice(32 * quadrant, 32 * quadrant + 4)
-            nc.vector.tensor_copy(tab_s[rows, :].bitcast(I32), landing[rows, :])
+        nc.sync.dma_start(landing[0:16, :], tab_scales[0].bitcast(I32))
+        nc.sync.dma_start(pick[:], offs)
+        nc.vector.tensor_copy(tab_s[0:16, :].bitcast(I32), landing[0:16, :])
         nc.gpsimd.dma_start(c0_rows[0:4, :], c0[0:512].rearrange("(s p) -> s p", p=P))
         make_identity(nc, ident[:])
         nc.scalar.activation(warm[1][:], warm[0][:], SQRT)
-        nc.sync.dma_start(w1_w[:].bitcast(I32), w1_words[0].bitcast(I32))
         load_w2(0)
-        nc.sync.dma_start(tab_w[:], tab_words[0].rearrange("p t i -> p (t i)").bitcast(I32))
-        for r in range(4):
-            nc.sync.dma_start(w1_s[r:P:32, :].bitcast(I32), w1_scales[0, r:16:4, :].bitcast(I32))
-        load_w2(1)
         nc.sync.dma_start(place[:], offs2)
+        nc.sync.dma_start(w1_w[:, 0:2 * P].bitcast(I32), w1_words[0][:, 0:2 * P].bitcast(I32))
+        for r in range(4):
+            if r == 2:
+                nc.sync.dma_start(tab_w[:], tab_words[0].rearrange("p t i -> p (t i)").bitcast(I32))
+            nc.sync.dma_start(w1_s[r:P:32, :].bitcast(I32), w1_scales[0, r:16:4, :].bitcast(I32))
+        nc.vector.tensor_copy(picked_s[:], tab_s[:].indirect(pick[:]))
+        for quadrant in (1, 2, 3):
+            nc.sync.dma_start(v_s[32 * quadrant:32 * quadrant + 4, :].bitcast(I32), picked_s[4 * quadrant:4 * quadrant + 4, :].bitcast(I32))
+        quantize_w2(0, 0, 0, P, nc.vector.tensor_copy)
+        nc.vector.tensor_copy(v_s[0:4, :].bitcast(I32), picked_s[0:4, :].bitcast(I32))
+        pages[0] = sb.tile([P, T2], F32, name="page0", tag="table scales", align_bytes=64)
+        load_w2(1)
         load_page(0)
-        nc.sync.dma_start(wgs_sb[:, 0:BANK], wgs[:, 0:BANK])
-        nc.sync.dma_start(wgs_sb[:, BANK:S], wgs[:, BANK:S])
-        load_page(1)
+        nc.sync.dma_start(wgs_sb[:, 0:2 * P], wgs[:, 0:2 * P])
+        load_w2(5)
+        nc.sync.dma_start(w1_w[:, 2 * P:2 * H].bitcast(I32), w1_words[0][:, 2 * P:2 * H].bitcast(I32))
+        nc.sync.dma_start(wgs_sb[:, 2 * P:S], wgs[:, 2 * P:S])
         load_w2(2)
+        load_page(1)
         load_w2(3)
+        load_w2(4)
         load_page(2)
         load_page(3)
         nc.sync.dma_start(c0_dealt[:], c0[512:1024].rearrange("(p t) -> p t", t=4))
@@ -150,37 +168,15 @@ def tile_list_floorplan_beacon_tiles_kernel(
         nc.tensor.transpose(banks[7][:, 0:P], c0_rows[:], ident[:])
         nc.scalar.copy(c0_cols[:], banks[7][:, 0:4])
 
-        nc.gpsimd.tensor_copy(
-            w1_s_dealt[:].rearrange("p (t q) -> p t q", t=4),
-            w1_s[:, BANK:H].rearrange("p (q t) -> p t q", t=4),
-        )
-
-        def quantize_w2(i, piece, a, b, copy):
-            start = W2_PIECES[piece][0]
-            rounded = w2_bf[i][:, 0:4 * (b - a)]
-            raw = w2_raw[piece].rearrange("p (t c) -> p t c", t=4)[:, :, a - start:b - start]
-            copy(rounded.rearrange("p (c i t) -> p c t i", i=4, t=4), raw.rearrange("p t (c i) -> p c t i", i=4))
-            if i > 0:
-                w2_w[i] = tenant("first roots" if i == 2 else "w2 codes", "w2_w" + str(i), [P, b - a], U32)
-            nc.vector.quantize_mx(w2_w[i].bitcast(FP8X4), w2_s[:, a:b], rounded)
-
         def deal_w2(i):
-            q0 = 64 * (i - 2)
+            q0 = 64 * (i - 3)
             nc.scalar.copy(
                 w2_dealt[:].rearrange("p (t q i) -> p q i t", t=4, i=4)[:, q0:q0 + 64],
                 w2_raw[i].rearrange("p (i q t) -> p q i t", i=4, t=4),
             )
 
-        quantize_w2(0, 0, 0, P, nc.scalar.copy)
-        nc.vector.tensor_copy(v_s[0][:], tab_s[:].indirect(pick[:, 0:32]))
-        for half in range(2):
-            nc.vector.tensor_copy(v_w[half][:], tab_w[:].bitcast(U32).indirect(pick[:, 32 * half:32 * (half + 1)]))
-        v_s.append(tenant("table words", "v_s1", [P, S // 2], U8))
-        nc.vector.tensor_copy(v_s[1], tab_s[:].indirect(pick[:, 32:64]))
-        nc.vector.tensor_copy(
-            w1_dealt.bitcast(U16).rearrange("p (t q) -> p t q", t=4),
-            w1_w[:, H:2 * H].bitcast(U16).rearrange("p (q t) -> p t q", t=4),
-        )
+        for (a, b), picked in zip(PICKS, v_w):
+            nc.vector.tensor_copy(picked[:], tab_w[:].bitcast(U32).indirect(pick[:, a // 16:b // 16]))
 
         ring = {"turn": 0, "square": 0, "grouped": 0}
 
@@ -192,24 +188,24 @@ def tile_list_floorplan_beacon_tiles_kernel(
         product_banks = banks[0:4]
         sum_banks = (banks[4:6], banks[6:8])
 
-        quantize_w2(1, 1, P, 2 * P, nc.scalar.copy)
-        h_first = tenant("first roots", "h_first", [P, 2 * P], F32)
+        quantize_w2(1, 1, P, 2 * P, nc.vector.tensor_copy)
+        h_first = [tenant("first roots" + str(n), "h_first" + str(n), [P, 2 * P], F32) for n in range(2)]
         h_0 = sb.tile([P, S], F32, name="h_0", align_bytes=64)[:]
         even, odd = (tenant("roots" + str(i), "h" + str(i), [P, S], F32) for i in range(2))
         h_of = [h_0, tenant("roots of tile 1", "h_1", [P, S], F32), even, odd, even, odd, even, odd]
 
         def roots_of(s, j_from, j_to):
-            return h_first if (s, j_from) == (0, 0) else h_of[s][:, j_from:j_to]
+            return h_first[j_from // (2 * P)] if s == 0 and j_from < BANK else h_of[s][:, j_from:j_to]
 
         def products(s, q, bank, sq=None, second_bank=None):
             if s < 4:
                 r_cols = slice(s * P, (s + 1) * P)
                 w1_codes, w1_plane = w1_w[:, 2 * s * P:2 * (s + 1) * P], w1_s[:, r_cols]
-                w2_codes = w2_w[s] if s < 2 else w2_w[2][:, (s - 2) * P:(s - 1) * P]
+                w2_codes = w2_w[s]
             else:
                 t = SLOT[s]
                 r_cols = slice(BANK + t * P, BANK + (t + 1) * P)
-                w1_codes, w1_plane = w1_dealt[:, 2 * t * P:2 * (t + 1) * P], w1_s_dealt[:, t * P:(t + 1) * P]
+                w1_codes, w1_plane = later["w1"][:, 2 * t * P:2 * (t + 1) * P], later["w1 scales"][:, t * P:(t + 1) * P]
                 w2_codes = later["w2"][:, t * P:(t + 1) * P]
             if sq is None:
                 sq = take("square", squares)[:]
@@ -218,8 +214,9 @@ def tile_list_floorplan_beacon_tiles_kernel(
                     nc.scalar.activation(sq[:, 0:2 * P], bank[:, 0:2 * P], SQUARE)
                     bank = second_bank
                 j = (2 * q + i) * P
-                words = v_w[j // BANK][:, j % BANK:j % BANK + P].bitcast(FP8X4)
-                plane = v_s[j // BANK][:, j % BANK:j % BANK + P]
+                piece = min(j // (2 * P), 2)
+                words = v_w[piece][:, j - PICKS[piece][0]:j - PICKS[piece][0] + P].bitcast(FP8X4)
+                plane = v_s[:, j:j + P]
                 nc.tensor.matmul_mx(
                     bank[:, (2 * i) * P:(2 * i + 1) * P], lhsT=words, lhsT_scale=plane,
                     rhs=w1_codes.bitcast(FP4X4), rhs_scale=w1_plane,
@@ -296,7 +293,7 @@ def tile_list_floorplan_beacon_tiles_kernel(
         def quantize_page(g, c):
             cols = slice(c * BANK, (c + 1) * BANK)
             ready = grouped[g][c]
-            nc.vector.quantize_mx(codes[g][c].bitcast(FP8X4), scales[g][:, cols], ready[:])
+            nc.vector.quantize_mx(codes[g][c].bitcast(FP8X4), scales[g][PLANE_ROW[g]:P, cols], ready[:])
 
         def store_codes(g, c_from, c_to):
             cols = slice(c_from * BANK, c_to * BANK)
@@ -307,14 +304,14 @@ def tile_list_floorplan_beacon_tiles_kernel(
 
         def store_scales(g):
             for r in range(4):
-                nc.sync.dma_start(out_3[g, r:16:4, :].bitcast(I32), scales[g][r:P:32, :].bitcast(I32))
+                nc.sync.dma_start(out_3[g, r:16:4, :].bitcast(I32), scales[g][PLANE_ROW[g] + r:P:32, :].bitcast(I32))
 
         def readout_pass(g, c, b, bank):
             cols = slice(c * BANK, (c + 1) * BANK)
             w_cols = slice(g * N + b * P, g * N + (b + 1) * P)
             nc.tensor.matmul_mx(
                 bank[:], lhsT=w3_w[:, w_cols].bitcast(FP8X4), lhsT_scale=w3_s[:, w_cols],
-                rhs=codes[g][c].bitcast(FP8X4), rhs_scale=scales[g][:, cols],
+                rhs=codes[g][c].bitcast(FP8X4), rhs_scale=scales[g][PLANE_ROW[g]:P, cols],
                 start=(g == 0), stop=(g == GROUPS - 1),
             )
 
@@ -347,28 +344,37 @@ def tile_list_floorplan_beacon_tiles_kernel(
                 round_into_pairs(s, c)
 
         for n in range(4):
-            add_squares([products(0, n, banks[n], w2_bf[2].bitcast(F32) if n == 1 else None, banks[6] if n == 0 else None)], banks[n + 2])
+            add_squares([products(0, n, banks[(0, 1, 6, 1)[n]], w2_bf[3].bitcast(F32) if n == 1 else None, banks[6] if n == 0 else None)], banks[n + 2])
             root(0, 256 * n, 256, banks[n + 2])
             if n != 2:
                 scatter(0, 256 * min(n, 2), 256 * (n + 1))
+            if n == 0:
+                later["w1 scales"] = tenant("dealt w1 scales", "w1_s_dealt", [P, BANK], U8)
+                nc.vector.tensor_copy(
+                    later["w1 scales"].rearrange("p (t q) -> p t q", t=4),
+                    w1_s[:, BANK:H].rearrange("p (q t) -> p t q", t=4),
+                )
+            if n == 2:
+                quantize_w2(2, 5, 2 * P, 3 * P, nc.scalar.copy)
             if n == 1:
-                quantize_w2(2, 1, 2 * P, 4 * P, nc.scalar.copy)
+                later["w1"] = tenant("dealt w1", "w1_dealt", [P, H], U8)
+                nc.vector.tensor_copy(
+                    later["w1"].bitcast(U16).rearrange("p (t q) -> p t q", t=4),
+                    w1_w[:, H:2 * H].bitcast(U16).rearrange("p (q t) -> p t q", t=4),
+                )
+        quantize_w2(3, 2, 3 * P, 4 * P, nc.scalar.copy)
         store_page(0)
-        all_sums(1, all_products(1, (None, None, None, w2_dealt[:, 0:2 * BANK].bitcast(F32))))
+        all_sums(1, [products(1, n, banks[(6, 1, 4, 5)[n]]) for n in range(4)])
         all_roots(1)
-        deal_w2(2)
+        all_sums(2, [products(2, n, banks[(1, 4, 5, 6)[n]], w2_dealt[:, 0:2 * BANK].bitcast(F32) if n == 3 else None) for n in range(4)])
         deal_w2(3)
-        all_sums(2, all_products(2))
+        deal_w2(4)
         last = TILES - 1
         for s in range(1, TILES):
-            if s == 1:
-                scatter(s, 0, BANK)
-                scatter(s, BANK, S)
-            else:
-                scatter(s, 0, S)
+            scatter(s, 0, S)
             store_page(s)
             if s == 1:
-                later["w2"] = tenant("roots of tile 1", "w2_w_dealt", [P, BANK], U32)
+                later["w2"] = tenant("dealt w2 codes", "w2_w_dealt", [P, BANK], U32)
                 nc.vector.quantize_mx(later["w2"].bitcast(FP8X4), w2_s[:, BANK:H], w2_dealt[:])
             if s < last:
                 all_roots(s + 1)
@@ -391,9 +397,10 @@ def tile_list_floorplan_beacon_tiles_kernel(
             if s >= 5:
                 round_tile(s - 1)
 
-        codes_1 = tenant("codes 1", "codes_1", [P, T2], U32)
+        codes_1 = tenant("table words", "codes_1", [P, T2], U32)
+        codes_0 = tenant("roots1", "codes_0", [P, T2], U32)
         code_pairs = [
-            [tenant("roots" + str(pair), "codes_0" + str(pair), [P, 2 * BANK], U32) for pair in range(2)],
+            [codes_0[:, 0:2 * BANK], codes_0[:, 2 * BANK:4 * BANK]],
             [codes_1[:, 0:2 * BANK], codes_1[:, 2 * BANK:4 * BANK]],
         ]
         for g in range(GROUPS):
@@ -406,7 +413,7 @@ def tile_list_floorplan_beacon_tiles_kernel(
                 store_codes(g, c, c + 1)
             elif c % 2 == 1:
                 store_codes(g, c - 1, c + 1)
-            if c + 1 == CHUNKS:
+            if g == 0 and c + 1 == CHUNKS:
                 store_scales(g)
 
         def store_out(b, c_from, c_to):
@@ -416,14 +423,15 @@ def tile_list_floorplan_beacon_tiles_kernel(
         for c in range(CHUNKS):
             round_into_pairs(last, c)
             join_pairs(c)
+        finish(1, 0)
         for c in range(CHUNKS):
             finish(0, c)
-        finish(1, 0)
         order = [(c, b) for c in range(CHUNKS) for b in range(NBLOCKS)]
         for n, (c, b) in enumerate(order):
-            bank = banks[n % 8]
+            bank = banks[n % (NBLOCKS + 1)]
             readout_pass(0, c, b, bank)
             readout_close(c, b, bank)
             store_out(b, c, c + 1)
             if b == 1 and c + 1 < CHUNKS:
                 finish(1, c + 1)
+        store_scales(1)

@@ -142,8 +142,13 @@ def tile_list_floorplan_beacon_tiles_kernel(
         load_w2(4)
         load_page(2)
         load_page(3)
+        parked = out_0.rearrange("n (h j) -> (n h) j", j=S)[0:4 * P, :]
+        nc.sync.dma_start(parked.rearrange("(c r) j -> r c j", c=4), wgs_sb[:].unsqueeze(1).to_broadcast([P, 4, S]))
         nc.sync.dma_start(c0_dealt[:], c0[512:1024].rearrange("(p t) -> p t", t=4))
         for s in range(4, TILES):
+            t = SLOT[s]
+            nc.sync.dma_start(wgs_dealt[:, t * S:(t + 1) * S], parked.rearrange("(p t) j -> t p j", t=4)[t])
+            load_page(s)
             if s == 7:
                 nc.sync.dma_start(
                     w3_w[:].rearrange("p (g n) -> p g n", g=GROUPS),
@@ -157,13 +162,6 @@ def tile_list_floorplan_beacon_tiles_kernel(
                 vis_sb.append(sb.tile([P, T2], F32, name="vis_last", tag="shared", align_bytes=64))
                 for b in range(NBLOCKS):
                     nc.sync.dma_start(vis_sb[b][:], vis[b * P:(b + 1) * P, :])
-            t = SLOT[s]
-            for quadrant in (0, 2, 1, 3):
-                nc.sync.dma_start(
-                    wgs_dealt[32 * quadrant:32 * (quadrant + 1), t * S:(t + 1) * S],
-                    wgs.rearrange("(q t) j -> t q j", t=4)[t],
-                )
-            load_page(s)
 
         nc.tensor.transpose(banks[7][:, 0:P], c0_rows[:], ident[:])
         nc.scalar.copy(c0_cols[:], banks[7][:, 0:4])
@@ -398,40 +396,42 @@ def tile_list_floorplan_beacon_tiles_kernel(
                 round_tile(s - 1)
 
         codes_1 = tenant("table words", "codes_1", [P, T2], U32)
-        codes_0 = tenant("roots1", "codes_0", [P, T2], U32)
         code_pairs = [
-            [codes_0[:, 0:2 * BANK], codes_0[:, 2 * BANK:4 * BANK]],
+            [tenant("roots1", "codes_0_first", [P, 2 * BANK], U32)],
             [codes_1[:, 0:2 * BANK], codes_1[:, 2 * BANK:4 * BANK]],
         ]
-        for g in range(GROUPS):
-            for c in range(CHUNKS):
-                codes[g][c] = code_pairs[g][c // 2][:, (c % 2) * BANK:(c % 2 + 1) * BANK]
-
-        def finish(g, c):
-            quantize_page(g, c)
-            if g == 1:
-                store_codes(g, c, c + 1)
-            elif c % 2 == 1:
-                store_codes(g, c - 1, c + 1)
-            if g == 0 and c + 1 == CHUNKS:
-                store_scales(g)
 
         def store_out(b, c_from, c_to):
             cols = slice(c_from * BANK, c_to * BANK)
             nc.sync.dma_start(out_0[b * P:(b + 1) * P, cols], vis_sb[b][:, cols])
 
+        def finish(g, c):
+            quantize_page(g, c)
+            if c % 2 == 1:
+                store_codes(g, c - 1, c + 1)
+            if g == 0 and c + 1 == CHUNKS:
+                store_scales(g)
+
         for c in range(CHUNKS):
             round_into_pairs(last, c)
             join_pairs(c)
+        code_pairs[0].append(tenant("stage0", "codes_0_second", [P, 2 * BANK], U32))
+        for g in range(GROUPS):
+            for c in range(CHUNKS):
+                codes[g][c] = code_pairs[g][c // 2][:, (c % 2) * BANK:(c % 2 + 1) * BANK]
         finish(1, 0)
         for c in range(CHUNKS):
             finish(0, c)
-        order = [(c, b) for c in range(CHUNKS) for b in range(NBLOCKS)]
+        finish(1, 1)
+        order = [(c0 + e, b) for c0 in (0, 2) for b in range(NBLOCKS) for e in range(2)]
         for n, (c, b) in enumerate(order):
             bank = banks[n % (NBLOCKS + 1)]
             readout_pass(0, c, b, bank)
             readout_close(c, b, bank)
-            store_out(b, c, c + 1)
-            if b == 1 and c + 1 < CHUNKS:
-                finish(1, c + 1)
+            if c % 2 == 1:
+                store_out(b, c - 1, c + 1)
+            if n == 1:
+                finish(1, 2)
+            if n == 4:
+                finish(1, 3)
         store_scales(1)

@@ -407,7 +407,9 @@ def tile_list_floorplan_beacon_tiles_kernel(
 
         def finish(g, c):
             quantize_page(g, c)
-            if c % 2 == 1:
+            if g == 1:
+                store_codes(g, c, c + 1)
+            elif c % 2 == 1:
                 store_codes(g, c - 1, c + 1)
             if g == 0 and c + 1 == CHUNKS:
                 store_scales(g)
@@ -422,16 +424,12 @@ def tile_list_floorplan_beacon_tiles_kernel(
         finish(1, 0)
         for c in range(CHUNKS):
             finish(0, c)
-        finish(1, 1)
-        order = [(c0 + e, b) for c0 in (0, 2) for b in range(NBLOCKS) for e in range(2)]
+        order = [(c, b) for c in range(CHUNKS) for b in range(NBLOCKS)]
         for n, (c, b) in enumerate(order):
             bank = banks[n % (NBLOCKS + 1)]
             readout_pass(0, c, b, bank)
             readout_close(c, b, bank)
-            if c % 2 == 1:
-                store_out(b, c - 1, c + 1)
-            if n == 1:
-                finish(1, 2)
-            if n == 4:
-                finish(1, 3)
+            store_out(b, c, c + 1)
+            if b == 1 and c + 1 < CHUNKS:
+                finish(1, c + 1)
         store_scales(1)

@@ -134,8 +134,9 @@ def tile_list_floorplan_beacon_tiles_kernel(
         load_page(0)
         nc.sync.dma_start(wgs_sb[:, 0:2 * P], wgs[:, 0:2 * P])
         load_w2(5)
+        nc.sync.dma_start(wgs_sb[:, 2 * P:BANK], wgs[:, 2 * P:BANK])
         nc.sync.dma_start(w1_w[:, 2 * P:2 * H].bitcast(I32), w1_words[0][:, 2 * P:2 * H].bitcast(I32))
-        nc.sync.dma_start(wgs_sb[:, 2 * P:S], wgs[:, 2 * P:S])
+        nc.sync.dma_start(wgs_sb[:, BANK:S], wgs[:, BANK:S])
         load_w2(2)
         load_page(1)
         load_w2(3)
@@ -430,6 +431,6 @@ def tile_list_floorplan_beacon_tiles_kernel(
             readout_pass(0, c, b, bank)
             readout_close(c, b, bank)
             store_out(b, c, c + 1)
-            if b == 1 and c + 1 < CHUNKS:
+            if b == 0 and c + 1 < CHUNKS:
                 finish(1, c + 1)
         store_scales(1)

@@ -26,7 +26,7 @@ CHUNKS = T2 // BANK
 NBLOCKS = N // P
 PLANE_ROW = (4, 0)
 SLOT = {4: 0, 5: 2, 6: 1, 7: 3}
-W2_PIECES = ((0, 128), (128, 256), (384, 512), (512, 768), (768, 1024), (256, 384))
+W2_PIECES = ((0, 128), (128, 256), (256, 512), (512, 768), (768, 1024))
 PICKS = ((0, 256), (256, 512), (512, 1024))
 
 
@@ -55,12 +55,12 @@ def tile_list_floorplan_beacon_tiles_kernel(
         w1_w = sb.tile([P, 2 * H], U8, name="w1_w", align_bytes=64)
         w1_s = sb.tile([P, H], U8, name="w1_s", align_bytes=64)
         stage = tiles("stage", CHUNKS, [P, 2 * BANK], F32)
-        w2_rest = sb.tile([P, BANK], F32, name="w2_rest", tag="codes 1", align_bytes=64)
-        w2_raw = [stage[0][:, 0:BANK], stage[0][:, 0:BANK], w2_rest[:], stage[2][:], stage[3][:], stage[1][:, 0:BANK]]
+        w2_raw = [stage[0][:, 0:BANK], stage[0][:, 0:BANK], stage[1][:], stage[2][:], stage[3][:]]
         w2_dealt = sb.tile([P, 4 * BANK], BF16, name="w2_dealt", tag="third", align_bytes=64)
         wgs_dealt = sb.tile([P, 4 * S], F32, name="wgs_dealt", align_bytes=64)
         c0_dealt = sb.tile([P, 4], F32, name="c0_dealt", align_bytes=64)
-        w2_w = {0: sb.tile([P, P], U32, name="w2_w0", align_bytes=64)[:]}
+        w2_w = {}
+        w2_first = tiles("w2_first", 2, [P, P], U32)
         w2_s = sb.tile([P, H], U8, name="w2_s", align_bytes=64)
         w3_w = sb.tile([P, GROUPS * N], I32, name="w3_w", align_bytes=64)
         w3_s = sb.tile([P, GROUPS * N], U8, name="w3_s", align_bytes=64)
@@ -93,14 +93,17 @@ def tile_list_floorplan_beacon_tiles_kernel(
             a, b = W2_PIECES[i]
             nc.sync.dma_start(w2_raw[i].rearrange("p (i c) -> p i c", i=4), w2[:, a:b].rearrange("(p i) c -> p i c", i=4))
 
-        def quantize_w2(i, piece, a, b, copy):
+        def round_w2(piece, a, b, copy):
             start = W2_PIECES[piece][0]
-            rounded = w2_bf[i][:, 0:4 * (b - a)]
+            rounded = w2_bf[piece][:, 4 * (a - start):4 * (b - start)]
             raw = w2_raw[piece].rearrange("p (t c) -> p t c", t=4)[:, :, a - start:b - start]
             copy(rounded.rearrange("p (c i t) -> p c t i", i=4, t=4), raw.rearrange("p t (c i) -> p c t i", i=4))
-            if i > 0:
-                w2_w[i] = tenant("first roots1" if i == 2 else "w2 codes" + str(i), "w2_w" + str(i), [P, b - a], U32)
-            nc.vector.quantize_mx(w2_w[i].bitcast(FP8X4), w2_s[:, a:b], rounded)
+
+        def quantize_w2(piece, codes_tile):
+            a, b = W2_PIECES[piece]
+            nc.vector.quantize_mx(codes_tile.bitcast(FP8X4), w2_s[:, a:b], w2_bf[piece][:, 0:4 * (b - a)])
+            for s in range(a // P, b // P):
+                w2_w[s] = codes_tile[:, s * P - a:(s + 1) * P - a]
 
         def rows_of(matrix, s):
             if s < 4:
@@ -127,17 +130,16 @@ def tile_list_floorplan_beacon_tiles_kernel(
         nc.vector.tensor_copy(picked_s[:], tab_s[:].indirect(pick[:]))
         for quadrant in (1, 2, 3):
             nc.sync.dma_start(v_s[32 * quadrant:32 * quadrant + 4, :].bitcast(I32), picked_s[4 * quadrant:4 * quadrant + 4, :].bitcast(I32))
-        quantize_w2(0, 0, 0, P, nc.vector.tensor_copy)
+        round_w2(0, 0, P, nc.vector.tensor_copy)
+        quantize_w2(0, w2_first[0][:])
         nc.vector.tensor_copy(v_s[0:4, :].bitcast(I32), picked_s[0:4, :].bitcast(I32))
         pages[0] = sb.tile([P, T2], F32, name="page0", tag="table scales", align_bytes=64)
         load_w2(1)
         load_page(0)
         nc.sync.dma_start(wgs_sb[:, 0:2 * P], wgs[:, 0:2 * P])
-        load_w2(5)
-        nc.sync.dma_start(wgs_sb[:, 2 * P:BANK], wgs[:, 2 * P:BANK])
-        nc.sync.dma_start(w1_w[:, 2 * P:2 * H].bitcast(I32), w1_words[0][:, 2 * P:2 * H].bitcast(I32))
-        nc.sync.dma_start(wgs_sb[:, BANK:S], wgs[:, BANK:S])
         load_w2(2)
+        nc.sync.dma_start(w1_w[:, 2 * P:2 * H].bitcast(I32), w1_words[0][:, 2 * P:2 * H].bitcast(I32))
+        nc.sync.dma_start(wgs_sb[:, 2 * P:S], wgs[:, 2 * P:S])
         load_page(1)
         load_w2(3)
         load_w2(4)
@@ -187,14 +189,14 @@ def tile_list_floorplan_beacon_tiles_kernel(
         product_banks = banks[0:4]
         sum_banks = (banks[4:6], banks[6:8])
 
-        quantize_w2(1, 1, P, 2 * P, nc.vector.tensor_copy)
-        h_first = [tenant("first roots" + str(n), "h_first" + str(n), [P, 2 * P], F32) for n in range(2)]
+        round_w2(1, P, 2 * P, nc.vector.tensor_copy)
+        quantize_w2(1, w2_first[1][:])
         h_0 = sb.tile([P, S], F32, name="h_0", align_bytes=64)[:]
         even, odd = (tenant("roots" + str(i), "h" + str(i), [P, S], F32) for i in range(2))
         h_of = [h_0, tenant("roots of tile 1", "h_1", [P, S], F32), even, odd, even, odd, even, odd]
 
         def roots_of(s, j_from, j_to):
-            return h_first[j_from // (2 * P)] if s == 0 and j_from < BANK else h_of[s][:, j_from:j_to]
+            return h_of[s][:, j_from:j_to]
 
         def products(s, q, bank, sq=None, second_bank=None):
             if s < 4:
@@ -343,29 +345,27 @@ def tile_list_floorplan_beacon_tiles_kernel(
                 round_into_pairs(s, c)
 
         for n in range(4):
-            add_squares([products(0, n, banks[(0, 1, 6, 1)[n]], w2_bf[3].bitcast(F32) if n == 1 else None, banks[6] if n == 0 else None)], banks[n + 2])
+            add_squares([products(0, n, banks[(0, 1, 6, 1)[n]], None, banks[6] if n == 0 else None)], banks[n + 2])
             root(0, 256 * n, 256, banks[n + 2])
-            if n != 2:
-                scatter(0, 256 * min(n, 2), 256 * (n + 1))
             if n == 0:
+                scatter(0, 0, 2 * P)
                 later["w1 scales"] = tenant("dealt w1 scales", "w1_s_dealt", [P, BANK], U8)
                 nc.vector.tensor_copy(
                     later["w1 scales"].rearrange("p (t q) -> p t q", t=4),
                     w1_s[:, BANK:H].rearrange("p (q t) -> p t q", t=4),
                 )
-            if n == 2:
-                quantize_w2(2, 5, 2 * P, 3 * P, nc.scalar.copy)
-            if n == 1:
+                round_w2(2, 2 * P, 4 * P, nc.vector.tensor_copy)
                 later["w1"] = tenant("dealt w1", "w1_dealt", [P, H], U8)
                 nc.vector.tensor_copy(
                     later["w1"].bitcast(U16).rearrange("p (t q) -> p t q", t=4),
                     w1_w[:, H:2 * H].bitcast(U16).rearrange("p (q t) -> p t q", t=4),
                 )
-        quantize_w2(3, 2, 3 * P, 4 * P, nc.scalar.copy)
+                quantize_w2(2, sb.tile([P, 2 * P], U32, name="w2_second", align_bytes=64)[:])
+        scatter(0, 2 * P, S)
         store_page(0)
         all_sums(1, [products(1, n, banks[(6, 1, 4, 5)[n]]) for n in range(4)])
         all_roots(1)
-        all_sums(2, [products(2, n, banks[(1, 4, 5, 6)[n]], w2_dealt[:, 0:2 * BANK].bitcast(F32) if n == 3 else None) for n in range(4)])
+        all_sums(2, [products(2, n, banks[(1, 6, 7, 1)[n]], w2_dealt[:, 0:2 * BANK].bitcast(F32) if n == 3 else None) for n in range(4)])
         deal_w2(3)
         deal_w2(4)
         last = TILES - 1

from contextlib import ExitStack

import concourse.mybir as mybir
from concourse.masks import make_identity

K, T, S, H, T2, N = 512, 4096, 1024, 1024, 2048, 384
FLOPS = 2 * (2 * K * H * S + H * N * T2)

F32 = mybir.dt.float32
BF16 = mybir.dt.bfloat16
I32 = mybir.dt.int32
U32 = mybir.dt.uint32
U16 = mybir.dt.uint16
U8 = mybir.dt.uint8
FP8X4 = mybir.dt.float8_e4m3fn_x4
FP4X4 = mybir.dt.float4_e2m1fn_x4
MULT = mybir.AluOpType.mult
SQUARE = mybir.ActivationFunctionType.Square
SQRT = mybir.ActivationFunctionType.Sqrt

P = 128
BANK = 512
TILES = H // P
GROUPS = H // 512
CHUNKS = T2 // BANK
NBLOCKS = N // P
PLANE_ROW = (4, 0)
SLOT = {4: 0, 5: 2, 6: 1, 7: 3}
W2_PIECES = ((0, 128), (128, 256), (256, 512), (512, 768), (768, 1024))
PICKS = ((0, 256), (256, 512), (512, 1024))


def tile_list_floorplan_beacon_tiles_kernel(
    tc, tab_words, tab_scales, offs, offs2, w1_words, w1_scales, w2, w3_words, w3_scales, c0, wgs, page0, vis,
    out_0, out_1, out_2, out_3,
):
    nc = tc.nc
    with ExitStack() as ctx:
        lists = ctx.enter_context(tc.tile_pool(name="lists", bufs=1))
        sb = ctx.enter_context(tc.tile_pool(name="sb", bufs=1))
        ps = ctx.enter_context(tc.psum_pool(name="ps", bufs=1))

        def tiles(name, count, shape, dtype):
            return [sb.tile(shape, dtype, name=name + str(i), align_bytes=64) for i in range(count)]

        pick = lists.tile([P, S // 16], U16, name="pick")
        place = lists.tile([P, S // 16], U16, name="place")
        banks = [ps.tile([P, BANK], F32, name="bank" + str(i)) for i in range(8)]

        tab_w = sb.tile([P, T], I32, name="tab_w", tag="table words", align_bytes=64)
        tab_s = sb.tile([P, T], U8, name="tab_s", tag="table scales", align_bytes=64)
        v_w = [sb.tile([P, b - a], U32, name="v_w" + str(a), align_bytes=64) for a, b in PICKS]
        picked_s = sb.tile([P, S], U8, name="picked_s", align_bytes=64)
        v_s = sb.tile([P, S], U8, name="v_s", align_bytes=64)
        w1_w = sb.tile([P, 2 * H], U8, name="w1_w", align_bytes=64)
        w1_s = sb.tile([P, H], U8, name="w1_s", align_bytes=64)
        stage = tiles("stage", CHUNKS, [P, 2 * BANK], F32)
        w2_raw = [stage[0][:, 0:BANK], stage[0][:, 0:BANK], stage[1][:], stage[2][:], stage[3][:]]
        w2_dealt = sb.tile([P, 4 * BANK], BF16, name="w2_dealt", tag="third", align_bytes=64)
        wgs_dealt = sb.tile([P, 4 * S], F32, name="wgs_dealt", align_bytes=64)
        c0_dealt = sb.tile([P, 4], F32, name="c0_dealt", align_bytes=64)
        w2_w = {}
        w2_first = tiles("w2_first", 2, [P, P], U32)
        w2_s = sb.tile([P, H], U8, name="w2_s", align_bytes=64)
        w3_w = sb.tile([P, GROUPS * N], I32, name="w3_w", align_bytes=64)
        w3_s = sb.tile([P, GROUPS * N], U8, name="w3_s", align_bytes=64)
        c0_rows = sb.tile([P, P], F32, name="c0_rows", align_bytes=64)
        c0_cols = sb.tile([P, 4], F32, name="c0_cols", align_bytes=64)
        ident = sb.tile([P, P], F32, name="ident", align_bytes=64)
        warm = tiles("warm", 2, [P, 1], F32)
        wgs_sb = sb.tile([P, S], F32, name="wgs_sb", align_bytes=64)
        pages = {s: sb.tile([P, T2], F32, name="page" + str(s), align_bytes=64) for s in range(1, TILES)}
        vis_sb = tiles("vis", NBLOCKS - 1, [P, T2], F32)
        squares = tiles("squares", 4, [P, BANK], F32)
        turned = tiles("turned", CHUNKS, [P, 4 * BANK], BF16)
        grouped = [tiles("grouped", CHUNKS, [P, 4 * BANK], BF16), turned]
        w2_bf = [grouped[0][c][:, 0:2 * BANK] for c in range(4)]
        later = {}
        codes = [{}, {}]

        def tenant(tag, name, shape, dtype):
            return sb.tile(shape, dtype, name=name, tag=tag, align_bytes=64)[:]
        scales = tiles("scales", GROUPS, [P, T2], U8)

        nc.gpsimd.memset(w1_s[:].bitcast(I32), 0)
        nc.vector.memset(tab_s[:].bitcast(I32), 0)
        nc.gpsimd.memset(c0_rows[:], 0.0)
        nc.vector.memset(warm[0][:], 1.0)
        nc.vector.memset(w3_s[:].bitcast(I32), 0)
        nc.vector.memset(v_s[:].bitcast(I32), 0)

        def load_w2(i):
            a, b = W2_PIECES[i]
            nc.sync.dma_start(w2_raw[i].rearrange("p (i c) -> p i c", i=4), w2[:, a:b].rearrange("(p i) c -> p i c", i=4))

        def round_w2(piece, a, b, copy):
            start = W2_PIECES[piece][0]
            rounded = w2_bf[piece][:, 4 * (a - start):4 * (b - start)]
            raw = w2_raw[piece].rearrange("p (t c) -> p t c", t=4)[:, :, a - start:b - start]
            copy(rounded.rearrange("p (c i t) -> p c t i", i=4, t=4), raw.rearrange("p t (c i) -> p c t i", i=4))

        def quantize_w2(piece, codes_tile):
            a, b = W2_PIECES[piece]
            nc.vector.quantize_mx(codes_tile.bitcast(FP8X4), w2_s[:, a:b], w2_bf[piece][:, 0:4 * (b - a)])
            for s in range(a // P, b // P):
                w2_w[s] = codes_tile[:, s * P - a:(s + 1) * P - a]

        def rows_of(matrix, s):
            if s < 4:
                return matrix[s * P:(s + 1) * P, :]
            return matrix[512:1024, :].rearrange("(p t) m -> t p m", t=4)[SLOT[s]]

        def load_page(s):
            nc.sync.dma_start(pages[s][:], rows_of(page0, s))

        landing = sb.tile([P, T // 4], I32, name="landing", tag="shared", align_bytes=64)
        nc.sync.dma_start(landing[0:16, :], tab_scales[0].bitcast(I32))
        nc.sync.dma_start(pick[:], offs)
        nc.vector.tensor_copy(tab_s[0:16, :].bitcast(I32), landing[0:16, :])
        nc.gpsimd.dma_start(c0_rows[0:4, :], c0[0:512].rearrange("(s p) -> s p", p=P))
        make_identity(nc, ident[:])
        nc.scalar.activation(warm[1][:], warm[0][:], SQRT)
        load_w2(0)
        nc.sync.dma_start(place[:], offs2)
        nc.sync.dma_start(w1_w[:, 0:2 * P].bitcast(I32), w1_words[0][:, 0:2 * P].bitcast(I32))
        for r in range(4):
            if r == 2:
                nc.sync.dma_start(tab_w[:], tab_words[0].rearrange("p t i -> p (t i)").bitcast(I32))
            nc.sync.dma_start(w1_s[r:P:32, :].bitcast(I32), w1_scales[0, r:16:4, :].bitcast(I32))
        nc.vector.tensor_copy(picked_s[:], tab_s[:].indirect(pick[:]))
        for quadrant in (1, 2, 3):
            nc.sync.dma_start(v_s[32 * quadrant:32 * quadrant + 4, :].bitcast(I32), picked_s[4 * quadrant:4 * quadrant + 4, :].bitcast(I32))
        round_w2(0, 0, P, nc.vector.tensor_copy)
        quantize_w2(0, w2_first[0][:])
        nc.vector.tensor_copy(v_s[0:4, :].bitcast(I32), picked_s[0:4, :].bitcast(I32))
        pages[0] = sb.tile([P, T2], F32, name="page0", tag="table scales", align_bytes=64)
        load_w2(1)
        load_page(0)
        nc.sync.dma_start(wgs_sb[:, 0:2 * P], wgs[:, 0:2 * P])
        load_w2(2)
        nc.sync.dma_start(w1_w[:, 2 * P:2 * H].bitcast(I32), w1_words[0][:, 2 * P:2 * H].bitcast(I32))
        nc.sync.dma_start(wgs_sb[:, 2 * P:S], wgs[:, 2 * P:S])
        load_page(1)
        load_w2(3)
        load_w2(4)
        load_page(2)
        load_page(3)
        parked = out_0.rearrange("n (h j) -> (n h) j", j=S)[0:4 * P, :]
        nc.sync.dma_start(parked.rearrange("(c r) j -> r c j", c=4), wgs_sb[:].unsqueeze(1).to_broadcast([P, 4, S]))
        nc.sync.dma_start(c0_dealt[:], c0[512:1024].rearrange("(p t) -> p t", t=4))
        for s in range(4, TILES):
            t = SLOT[s]
            nc.sync.dma_start(wgs_dealt[:, t * S:(t + 1) * S], parked.rearrange("(p t) j -> t p j", t=4)[t])
            load_page(s)
            if s == 7:
                nc.sync.dma_start(
                    w3_w[:].rearrange("p (g n) -> p g n", g=GROUPS),
                    w3_words.rearrange("g p n t -> p g (n t)").bitcast(I32),
                )
                for r in range(4):
                    nc.sync.dma_start(
                        w3_s[r:P:32, :].bitcast(I32).rearrange("q (g n) -> q g n", g=GROUPS),
                        w3_scales.bitcast(I32)[:, r:16:4, :].rearrange("g q n -> q g n"),
                    )
                vis_sb.append(sb.tile([P, T2], F32, name="vis_last", tag="shared", align_bytes=64))
                for b in range(NBLOCKS):
                    nc.sync.dma_start(vis_sb[b][:], vis[b * P:(b + 1) * P, :])

        nc.tensor.transpose(banks[7][:, 0:P], c0_rows[:], ident[:])
        nc.scalar.copy(c0_cols[:], banks[7][:, 0:4])

        def deal_w2(i):
            q0 = 64 * (i - 3)
            nc.scalar.copy(
                w2_dealt[:].rearrange("p (t q i) -> p q i t", t=4, i=4)[:, q0:q0 + 64],
                w2_raw[i].rearrange("p (i q t) -> p q i t", i=4, t=4),
            )

        for (a, b), picked in zip(PICKS, v_w):
            nc.vector.tensor_copy(picked[:], tab_w[:].bitcast(U32).indirect(pick[:, a // 16:b // 16]))

        ring = {"turn": 0, "square": 0, "grouped": 0}

        def take(kind, items):
            item = items[ring[kind] % len(items)]
            ring[kind] = ring[kind] + 1
            return item

        product_banks = banks[0:4]
        sum_banks = (banks[4:6], banks[6:8])

        round_w2(1, P, 2 * P, nc.vector.tensor_copy)
        quantize_w2(1, w2_first[1][:])
        h_0 = sb.tile([P, S], F32, name="h_0", align_bytes=64)[:]
        even, odd = (tenant("roots" + str(i), "h" + str(i), [P, S], F32) for i in range(2))
        h_of = [h_0, tenant("roots of tile 1", "h_1", [P, S], F32), even, odd, even, odd, even, odd]

        def roots_of(s, j_from, j_to):
            return h_of[s][:, j_from:j_to]

        def products(s, q, bank, sq=None, second_bank=None):
            if s < 4:
                r_cols = slice(s * P, (s + 1) * P)
                w1_codes, w1_plane = w1_w[:, 2 * s * P:2 * (s + 1) * P], w1_s[:, r_cols]
                w2_codes = w2_w[s]
            else:
                t = SLOT[s]
                r_cols = slice(BANK + t * P, BANK + (t + 1) * P)
                w1_codes, w1_plane = later["w1"][:, 2 * t * P:2 * (t + 1) * P], later["w1 scales"][:, t * P:(t + 1) * P]
                w2_codes = later["w2"][:, t * P:(t + 1) * P]
            if sq is None:
                sq = take("square", squares)[:]
            for i in range(2):
                if i == 1 and second_bank is not None:
                    nc.scalar.activation(sq[:, 0:2 * P], bank[:, 0:2 * P], SQUARE)
                    bank = second_bank
                j = (2 * q + i) * P
                piece = min(j // (2 * P), 2)
                words = v_w[piece][:, j - PICKS[piece][0]:j - PICKS[piece][0] + P].bitcast(FP8X4)
                plane = v_s[:, j:j + P]
                nc.tensor.matmul_mx(
                    bank[:, (2 * i) * P:(2 * i + 1) * P], lhsT=words, lhsT_scale=plane,
                    rhs=w1_codes.bitcast(FP4X4), rhs_scale=w1_plane,
                    start=True, stop=True,
                )
                nc.tensor.matmul_mx(
                    bank[:, (2 * i + 1) * P:(2 * i + 2) * P], lhsT=words, lhsT_scale=plane,
                    rhs=w2_codes.bitcast(FP8X4), rhs_scale=w2_s[:, r_cols],
                    start=True, stop=True,
                )
            first = 0 if second_bank is None else 2 * P
            nc.scalar.activation(sq[:, first:BANK], bank[:, first:BANK], SQUARE)
            return sq

        def add_squares(made, total):
            for n, sq in enumerate(made):
                for i in range(2):
                    dst = total[:, (2 * n + i) * P:(2 * n + i + 1) * P]
                    for part in range(2):
                        nc.tensor.matmul(
                            dst, lhsT=sq[:, (2 * i + part) * P:(2 * i + part + 1) * P], rhs=ident[:],
                            start=(part == 0), stop=(part == 1), is_transpose=True,
                        )

        def root(s, j0, width, total):
            bias = c0_cols[:, s:s + 1] if s < 4 else c0_dealt[:, SLOT[s]:SLOT[s] + 1]
            nc.scalar.activation(roots_of(s, j0, j0 + width), total[:, 0:width], SQRT, bias=bias)

        def scatter(s, j_from, j_to):
            factor = wgs_sb[:] if s < 4 else wgs_dealt[:, SLOT[s] * S:(SLOT[s] + 1) * S]
            nc.vector.tensor_tensor(
                pages[s][:].indirect(place[:, j_from // 16:j_to // 16]),
                roots_of(s, j_from, j_to), factor[:, j_from:j_to], MULT,
            )

        def store_page(s):
            nc.sync.dma_start(rows_of(out_1, s), pages[s][:])

        def turn(s, c, copy, bank):
            for mb in range(4):
                m0 = c * BANK + mb * P
                nc.tensor.transpose(bank[:, mb * P:(mb + 1) * P], pages[s][:, m0:m0 + P], ident[:])
            q0 = 32 * (s % 4)
            copy(
                turned[c][:].rearrange("m (b u p e) -> m b u p e", b=4, u=2, e=2)[:, :, :, q0:q0 + 32, :],
                bank[:].rearrange("m (b q u e) -> m b u q e", b=4, u=2, e=2),
            )

        def turn_back(c, copies, into):
            ready = grouped[0][c]
            words = turned[c][:].bitcast(F32)
            for half in range(2):
                bank = into[half]
                for i in range(4):
                    w0 = (4 * half + i) * P
                    nc.tensor.transpose(bank[:, i * P:(i + 1) * P], words[:, w0:w0 + P], ident[:])
                copies[half](
                    ready[:].bitcast(F32)[:, half * BANK:(half + 1) * BANK].rearrange("p (b m u) -> p b m u", b=2, u=2),
                    bank[:].rearrange("p (b u m) -> p b m u", b=2, u=2),
                )

        def round_into_pairs(s, c):
            u, e = divmod(SLOT[s], 2)
            pairs = stage[c][:].bitcast(BF16).rearrange("p (u m e) -> p u m e", u=2, e=2)
            nc.scalar.copy(pairs[:, u, :, e], pages[s][:, c * BANK:(c + 1) * BANK])

        def join_pairs(c):
            copy, word = (nc.vector.tensor_copy, I32) if c == 0 else (nc.scalar.copy, U32)
            copy(
                grouped[1][c][:].bitcast(word).rearrange("p (m u) -> p m u", u=2),
                stage[c][:].bitcast(word).rearrange("p (u m) -> p m u", u=2),
            )

        def quantize_page(g, c):
            cols = slice(c * BANK, (c + 1) * BANK)
            ready = grouped[g][c]
            nc.vector.quantize_mx(codes[g][c].bitcast(FP8X4), scales[g][PLANE_ROW[g]:P, cols], ready[:])

        def store_codes(g, c_from, c_to):
            cols = slice(c_from * BANK, c_to * BANK)
            within = slice((c_from % 2) * BANK, (c_from % 2 + c_to - c_from) * BANK)
            nc.sync.dma_start(
                out_2[g].rearrange("p m t -> p (m t)").bitcast(I32)[:, cols], code_pairs[g][c_from // 2][:, within].bitcast(I32)
            )

        def store_scales(g):
            for r in range(4):
                nc.sync.dma_start(out_3[g, r:16:4, :].bitcast(I32), scales[g][PLANE_ROW[g] + r:P:32, :].bitcast(I32))

        def readout_pass(g, c, b, bank):
            cols = slice(c * BANK, (c + 1) * BANK)
            w_cols = slice(g * N + b * P, g * N + (b + 1) * P)
            nc.tensor.matmul_mx(
                bank[:], lhsT=w3_w[:, w_cols].bitcast(FP8X4), lhsT_scale=w3_s[:, w_cols],
                rhs=codes[g][c].bitcast(FP8X4), rhs_scale=scales[g][PLANE_ROW[g]:P, cols],
                start=(g == 0), stop=(g == GROUPS - 1),
            )

        def readout_close(c, b, bank):
            cols = slice(c * BANK, (c + 1) * BANK)
            readout_pass(1, c, b, bank)
            nc.vector.tensor_tensor(vis_sb[b][:, cols], bank[:], vis_sb[b][:, cols], MULT)


        s_copy = nc.scalar.copy
        v_copy = nc.vector.tensor_copy

        def all_products(s, held=(None, None, None, None)):
            return [products(s, n, product_banks[n], held[n]) for n in range(4)]

        def all_sums(s, made):
            for half in range(2):
                add_squares(made[2 * half:2 * half + 2], sum_banks[s % 2][half])

        def all_roots(s):
            for half in range(2):
                root(s, half * BANK, BANK, sum_banks[s % 2][half])

        def turn_tile(s):
            for c in range(CHUNKS):
                turn(s, c, s_copy, product_banks[c])

        def round_tile(s):
            for c in range(CHUNKS):
                round_into_pairs(s, c)

        for n in range(4):
            add_squares([products(0, n, banks[(0, 1, 6, 1)[n]], None, banks[6] if n == 0 else None)], banks[n + 2])
            root(0, 256 * n, 256, banks[n + 2])
            if n == 0:
                scatter(0, 0, 2 * P)
                later["w1 scales"] = tenant("dealt w1 scales", "w1_s_dealt", [P, BANK], U8)
                nc.vector.tensor_copy(
                    later["w1 scales"].rearrange("p (t q) -> p t q", t=4),
                    w1_s[:, BANK:H].rearrange("p (q t) -> p t q", t=4),
                )
                round_w2(2, 2 * P, 4 * P, nc.vector.tensor_copy)
                later["w1"] = tenant("dealt w1", "w1_dealt", [P, H], U8)
                nc.vector.tensor_copy(
                    later["w1"].bitcast(U16).rearrange("p (t q) -> p t q", t=4),
                    w1_w[:, H:2 * H].bitcast(U16).rearrange("p (q t) -> p t q", t=4),
                )
                quantize_w2(2, sb.tile([P, 2 * P], U32, name="w2_second", align_bytes=64)[:])
        scatter(0, 2 * P, S)
        store_page(0)
        all_sums(1, [products(1, n, banks[(6, 1, 4, 5)[n]]) for n in range(4)])
        all_roots(1)
        all_sums(2, [products(2, n, banks[(1, 6, 7, 1)[n]], w2_dealt[:, 0:2 * BANK].bitcast(F32) if n == 3 else None) for n in range(4)])
        deal_w2(3)
        deal_w2(4)
        last = TILES - 1
        for s in range(1, TILES):
            scatter(s, 0, S)
            store_page(s)
            if s == 1:
                later["w2"] = tenant("dealt w2 codes", "w2_w_dealt", [P, BANK], U32)
                nc.vector.quantize_mx(later["w2"].bitcast(FP8X4), w2_s[:, BANK:H], w2_dealt[:])
            if s < last:
                all_roots(s + 1)
            made = None
            if s in (4, 5):
                made = all_products(s + 2, [stage[c][:, (s - 4) * BANK:(s - 3) * BANK] for c in range(CHUNKS)])
            elif s < 4:
                made = all_products(s + 2)
            if s <= 4:
                turn_tile(s - 1)
            if made is not None:
                all_sums(s + 2, made)
            if s == 4:
                turn_back(0, (s_copy, s_copy), product_banks[0:2])
            if s == 6:
                turn_back(1, (s_copy, s_copy), product_banks[0:2])
                turn_back(2, (s_copy, s_copy), product_banks[2:4])
            if s == last:
                turn_back(3, (s_copy, s_copy), sum_banks[0])
            if s >= 5:
                round_tile(s - 1)

        codes_1 = tenant("table words", "codes_1", [P, T2], U32)
        code_pairs = [
            [tenant("roots1", "codes_0_first", [P, 2 * BANK], U32)],
            [codes_1[:, 0:2 * BANK], codes_1[:, 2 * BANK:4 * BANK]],
        ]

        def store_out(b, c_from, c_to):
            cols = slice(c_from * BANK, c_to * BANK)
            nc.sync.dma_start(out_0[b * P:(b + 1) * P, cols], vis_sb[b][:, cols])

        def finish(g, c):
            quantize_page(g, c)
            if g == 1:
                store_codes(g, c, c + 1)
            elif c % 2 == 1:
                store_codes(g, c - 1, c + 1)
            if g == 0 and c + 1 == CHUNKS:
                store_scales(g)

        for c in range(CHUNKS):
            round_into_pairs(last, c)
            join_pairs(c)
        code_pairs[0].append(tenant("stage0", "codes_0_second", [P, 2 * BANK], U32))
        for g in range(GROUPS):
            for c in range(CHUNKS):
                codes[g][c] = code_pairs[g][c // 2][:, (c % 2) * BANK:(c % 2 + 1) * BANK]
        finish(1, 0)
        for c in range(CHUNKS):
            finish(0, c)
        order = [(c, b) for c in range(CHUNKS) for b in range(NBLOCKS)]
        for n, (c, b) in enumerate(order):
            bank = banks[n % (NBLOCKS + 1)]
            readout_pass(0, c, b, bank)
            readout_close(c, b, bank)
            store_out(b, c, c + 1)
            if b == 0 and c + 1 < CHUNKS:
                finish(1, c + 1)
        store_scales(1)
